import numpy as np
import ml_dtypes


def mxq(x, axis, fmt="e4m3"):
    dtype, down = {"e4m3": (ml_dtypes.float8_e4m3fn, 7), "e5m2": (ml_dtypes.float8_e5m2, 14)}[fmt]
    v = np.moveaxis(np.asarray(x, np.float32).astype(ml_dtypes.bfloat16).astype(np.float64), axis, -1)
    blocks = v.reshape(v.shape[:-1] + (-1, 32))
    amax = np.abs(blocks).max(-1, keepdims=True)
    byte = np.maximum(np.where(amax > 0, np.frexp(amax)[1] - 1 + 127, 0) - down, 1)
    scale = np.exp2(byte - 127.0)
    codes = (blocks / scale).astype(np.float32).astype(dtype).astype(np.float64)
    return np.moveaxis((codes * scale).reshape(v.shape), -1, axis)


WIDE = False


def mx_kscale(k):
    if not WIDE:
        return np.ones(k)
    levels = np.array([10, -10, 5, -5, 0])
    if k % 512:
        return np.exp2(np.random.permutation(np.resize(levels, k // 32))).repeat(32)
    a = np.empty((k // 512, 16))
    for p in range(k // 512):
        a[p, :8] = np.random.permutation(np.resize(levels, 8))
        for g in range(8):
            far = levels[np.abs(levels - a[p, g]) >= 10]
            a[p, g + 8] = far[np.random.randint(len(far))]
    return np.exp2(a.ravel()).repeat(32)


BF16 = ml_dtypes.bfloat16


def bf(x):
    return np.asarray(x, np.float32).astype(BF16)


def f64(x):
    return np.asarray(x).astype(np.float64)


R, N, D, C, M, J = 1024, 1024, 1024, 512, 4, 7


def density_projection(h, w, e):
    u = mxq(f64(h), 1, "e4m3") @ mxq(f64(w), 0, "e4m3")
    return mxq(f64(e), 2, "e4m3") @ mxq(u, 0, "e4m3")


def draw0():
    s = mx_kscale(D)
    t = mx_kscale(N)
    h = np.random.standard_normal((N, D)) * s[None, :] * t[:, None]
    w = np.random.standard_normal((D, C)) / np.sqrt(D) / s[:, None]
    e = np.random.standard_normal((M, R, N)) / np.sqrt(N) / t[None, None, :]
    coef = np.random.standard_normal((J, C)) * 0.4
    return {"h": bf(h), "w": bf(w), "e": bf(e), "coef": bf(coef)}


def core(h, w, e, coef):
    am = density_projection(h, w, e)
    coef = f64(coef)

    s = am[0]
    t = (am[1] ** 2 + am[2] ** 2 + am[3] ** 2) / 3.0

    b0 = (coef[0][None, :] * s
          + coef[1][None, :] * s ** 2
          + coef[2][None, :] * t
          + coef[3][None, :] * s * t)

    q = coef[4][None, :] + coef[5][None, :] * s + coef[6][None, :] * t
    b1 = am[1] * q
    b2 = am[2] * q
    b3 = am[3] * q

    return np.stack([b0, b1, b2, b3], axis=0)


def e4m3fn_bytes(y):
    return np.clip(np.asarray(y, np.float64), -448.0, 448.0).astype(np.float32).astype(ml_dtypes.float8_e4m3fn).view(np.uint8)


def e4m3fn_values(b):
    return np.asarray(b, np.uint8).view(ml_dtypes.float8_e4m3fn).astype(np.float64)


def setup_inputs():
    d = draw0()
    x0 = np.asarray(d['e']).astype(np.float64)
    s = (np.max(np.abs(x0), axis=(0, 1), keepdims=True) / 448.0).astype(np.float32)
    out = {}
    for k, v in d.items():
        if k == 'e':
            out['e_bytes'] = e4m3fn_bytes(x0 / s.astype(np.float64))
            out['e_scale'] = s
        else:
            out[k] = v
    return out


def reference(h, w, e_bytes, e_scale, coef):
    return core(h, w, e4m3fn_values(e_bytes) * e_scale.astype(np.float64), coef)

@@ -1,0 +1,451 @@
+from contextlib import ExitStack
+
+import concourse.mybir as mybir
+from concourse.masks import make_identity
+
+R, N, D, C, M, J = 1024, 1024, 1024, 512, 4, 7
+FLOPS = 2 * N * D * C + 2 * M * R * N * C
+
+F32 = mybir.dt.float32
+BF16 = mybir.dt.bfloat16
+U32 = mybir.dt.uint32
+U8 = mybir.dt.uint8
+FP8 = mybir.dt.float8_e4m3fn
+FP8X4 = mybir.dt.float8_e4m3fn_x4
+ALU = mybir.AluOpType
+ACT = mybir.ActivationFunctionType
+
+P = 128
+G = 2
+KP = 512
+CB = C // P
+RB = R // P
+TAILV = 6
+
+
+def tile_macedensitytricksymmetriccontraction_kernel(tc, h, w, e_bytes, e_scale, coef, out):
+    nc = tc.nc
+    with ExitStack() as ctx:
+        keep = ctx.enter_context(tc.tile_pool(name="keep", bufs=1))
+        work = ctx.enter_context(tc.tile_pool(name="work", bufs=2))
+        psum = ctx.enter_context(tc.psum_pool(name="psum", bufs=1))
+        ctx.enter_context(tc.manual_schedule())
+
+        turns = []
+
+        def bank_at(i):
+            return psum.tile([P, 512], F32, name="bank%d" % i, tag="bank%d" % i)
+
+        def rot_bank():
+            turns.append(None)
+            return bank_at(3 + len(turns) % 5)
+
+        scale_col = keep.tile([P, G, 4], F32, name="scale_col")
+        nc.sync.dma_start(out=scale_col[:], in_=e_scale[0, 0, :].rearrange("(g p t) -> p g t", g=G, t=4))
+        coef_rows = keep.tile([J * CB, P], BF16, name="coef_rows")
+        nc.sync.dma_start(out=coef_rows[:], in_=coef.rearrange("j (b p) -> (j b) p", p=P))
+
+        w_raw, h_raw, ea_bytes, es_bytes = {}, {}, {}, {}
+
+        def load_w(g):
+            w_raw[g] = keep.tile([P, 4, C], BF16, name="w_raw%d" % g)
+            nc.sync.dma_start(out=w_raw[g][:], in_=w[g * KP:(g + 1) * KP, :].rearrange("(p t) c -> p t c", t=4))
+
+        def load_h(g, half):
+            h_raw[g, half] = keep.tile([P, 2 * D], BF16, name="h_raw%d_%d" % (g, half))
+            rows = h[g * KP:(g + 1) * KP, :].rearrange("(p s t) d -> p s (t d)", s=2, t=2)
+            nc.sync.dma_start(out=h_raw[g, half][:], in_=rows[:, half, :])
+
+        def load_ea(rb):
+            ea_bytes[rb] = keep.tile([P, M - 1, N], U8, name="ea_bytes%d" % rb)
+            nc.sync.dma_start(out=ea_bytes[rb][:], in_=e_bytes[1:M, rb * P:(rb + 1) * P, :].rearrange("m r k -> r m k"))
+
+        def load_es(pair):
+            es_bytes[pair] = keep.tile([P, 2, N], U8, name="es_bytes%d" % pair)
+            nc.sync.dma_start(out=es_bytes[pair][:],
+                              in_=e_bytes[0, pair * 2 * P:(pair + 1) * 2 * P, :].rearrange("(b r) k -> r b k", b=2))
+
+        load_w(0)
+        load_ea(0)
+        load_h(0, 0)
+        load_h(0, 1)
+        load_w(1)
+        load_h(1, 0)
+        load_es(0)
+        load_h(1, 1)
+        load_ea(1)
+        load_es(1)
+        for rb in range(2, RB):
+            load_ea(rb)
+            if rb < 4:
+                load_es(rb)
+
+        ident = keep.tile([P, P], F32, name="ident")
+        make_identity(nc, ident[:])
+        coef_pad = keep.tile([P, P], F32, name="coef_pad")
+        nc.vector.memset(coef_pad[:], 0.0)
+        warm = keep.tile([P, 1], F32, name="warm")
+        nc.scalar.activation(out=warm[:], in_=coef_pad[:, 0:1], func=ACT.Square)
+        scale_row = keep.tile([P, N], F32, name="scale_row")
+        coef_col = keep.tile([P, J * CB], F32, name="coef_col")
+
+        def spread_scale(g):
+            bank = rot_bank()
+            for t in range(4):
+                nc.tensor.transpose(bank[:, t * P:(t + 1) * P], scale_col[:, g, t:t + 1].to_broadcast([P, P]), ident[:])
+            nc.vector.tensor_copy(out=scale_row[:, g * KP:(g + 1) * KP].rearrange("q (p t) -> q p t", t=4),
+                                  in_=bank[:].rearrange("q (t p) -> q p t", t=4))
+
+        def turn_coef():
+            bank = rot_bank()
+            nc.tensor.transpose(bank[:, 0:P], coef_pad[:], ident[:])
+            nc.vector.tensor_copy(out=coef_col[:], in_=bank[:, 0:J * CB])
+
+        def cf(j, cb):
+            return coef_col[:, j * CB + cb:j * CB + cb + 1]
+
+        def quantize(name, src, bufs=1):
+            width = src.shape[1] // 4
+            codes = keep.tile([P, width], U32, name=name + "_codes", tag=name + "_codes", bufs=bufs, align_bytes=64)
+            scales = keep.tile([P, width], U8, name=name + "_scales", tag=name + "_scales", bufs=bufs, align_bytes=64)
+            nc.vector.quantize_mx(out=codes[:].bitcast(FP8X4), scales=scales[:], in_=src)
+            return codes, scales
+
+        def mx(dst, lhs, lcols, rhs, rcols, g):
+            nc.tensor.matmul_mx(out=dst, lhsT=lhs[0][:, lcols].bitcast(FP8X4), lhsT_scale=lhs[1][:, lcols],
+                                rhs=rhs[0][:, rcols].bitcast(FP8X4), rhs_scale=rhs[1][:, rcols],
+                                start=(g == 0), stop=(g == G - 1))
+
+        def cols(i, n):
+            return slice(i * n, (i + 1) * n)
+
+        def turn_rows(rows, bank):
+            words = rows.bitcast(F32)
+            for g in range(G):
+                for u in range(2):
+                    nc.tensor.transpose(bank[:, cols(2 * g + u, P)], words[:, 256 * g + u:256 * (g + 1):2], ident[:])
+            return bank
+
+        def empty_turned(bank, dst_words):
+            nc.scalar.copy(out=dst_words, in_=bank[:].rearrange("p (g u r) -> p g r u", g=G, u=2))
+
+        w_in, w_q, h_in, h_q, h_bank, u_in, u_q, u_bank = {}, {}, {}, {}, {}, {}, {}, {}
+
+        def w_interleave(g, copy):
+            w_in[g] = keep.tile([P, 4 * C], BF16, name="w_in%d" % g, tag="wu_in%d" % g, align_bytes=64)
+            copy(out=w_in[g][:].rearrange("p (c i t) -> p c t i", i=4, t=4),
+                 in_=w_raw[g][:].rearrange("p t (c i) -> p c t i", i=4))
+
+        def w_quant(g):
+            w_q[g] = quantize("w%d" % g, w_in[g][:])
+
+        def h_slab(g, t):
+            half = t // 2
+            if t % 2 == 0:
+                h_in[g, half] = keep.tile([P, 2 * D], BF16, name="h_in%d_%d" % (g, half), align_bytes=64)
+            bank = turn_rows(h_raw[g, half][:, cols(t % 2, D)], rot_bank())
+            dst = h_in[g, half][:, cols(t % 2, D)].bitcast(F32).rearrange("p (g r u) -> p g r u", g=G, u=2)
+            empty_turned(bank, dst)
+
+        def h_quant(g, half):
+            h_q[g, half] = quantize("h%d_%d" % (g, half), h_in[g, half][:])
+
+        def u_block(g, cb, bank):
+            if cb == 0:
+                u_in[g] = keep.tile([P, 4 * C], BF16, name="u_in%d" % g, tag="wu_in%d" % g, align_bytes=64)
+            for t in range(4):
+                for dg in range(G):
+                    mx(bank[:, cols(t, P)], h_q[g, t // 2], cols((t % 2) * G + dg, P), w_q[dg], cols(cb, P), dg)
+            nc.scalar.copy(out=u_in[g][:, cols(cb, 4 * P)].rearrange("p (c t) -> p c t", t=4),
+                           in_=bank[:].rearrange("p (t c) -> p c t", t=4))
+
+        def u_quant(g):
+            u_q[g] = quantize("u%d" % g, u_in[g][:])
+
+        e_val, e_bank, e_in, e_q = {}, {}, {}, {}
+
+        def e_scale_up(m, rb):
+            src = es_bytes[rb // 2][:, rb % 2, :] if m == 0 else ea_bytes[rb][:, m - 1, :]
+            e_val[m, rb] = work.tile([P, N], BF16, name="e_val", tag="e_val", bufs=6)
+            nc.vector.tensor_tensor(out=e_val[m, rb][:], in0=src.bitcast(FP8), in1=scale_row[:], op=ALU.mult)
+
+        def e_turn(m, rb, at=None):
+            e_bank[m, rb] = turn_rows(e_val[m, rb][:], rot_bank() if at is None else bank_at(at))
+
+        def e_empty(m, rb):
+            if m == 0:
+                if rb % 2 == 0:
+                    e_in[0, rb // 2] = work.tile([P, 2 * N], BF16, name="es_in", tag="es_in", bufs=2, align_bytes=64)
+                words = e_in[0, rb // 2][:].bitcast(F32).rearrange("p (g r u) -> p g r u", g=G, u=2)
+                dst = words[:, :, cols(rb % 2, P), :]
+            else:
+                e_in[m, rb] = work.tile([P, N], BF16, name="ea_in", tag="ea_in", bufs=6, align_bytes=64)
+                dst = e_in[m, rb][:].bitcast(F32).rearrange("p (g r u) -> p g r u", g=G, u=2)
+            empty_turned(e_bank[m, rb], dst)
+
+        def e_quant(m, rb):
+            if m == 0:
+                if rb % 2 == 1:
+                    e_q[0, rb // 2] = quantize("es", e_in[0, rb // 2][:], 2)
+            else:
+                e_q[m, rb] = quantize("ea", e_in[m, rb][:], 9)
+
+        s_bank, lin_a, lin_b, lin_q, p1 = {}, {}, {}, {}, {}
+
+        def s_matmul(pair, half, at):
+            bank = s_bank[pair, half] = bank_at(at)
+            for b in range(2):
+                for g in range(G):
+                    mx(bank[:, cols(b, 2 * P)], u_q[g], cols(2 * half + b, P), e_q[0, pair], cols(g, 2 * P), g)
+
+        def pair_tile(store, name, pair, half):
+            if half == 0:
+                store[pair] = work.tile([P, CB, 2 * P], F32, name=name, tag=name)
+            return store[pair][:, 2 * half:2 * half + 2, :]
+
+        def s_affine(store, name, j0, j1, pair, half):
+            dst = pair_tile(store, name, pair, half)
+            for b in range(2):
+                cb = 2 * half + b
+                nc.scalar.activation(out=dst[:, b, :], in_=s_bank[pair, half][:, cols(b, 2 * P)],
+                                     func=ACT.Identity, scale=cf(j1, cb), bias=cf(j0, cb))
+
+        def s_linear(pair, half):
+            lin_a[pair, half] = work.tile([P, 512], F32, name="lin_a", tag="lin_a")
+            for b in range(2):
+                cb = 2 * half + b
+                nc.scalar.activation(out=lin_a[pair, half][:, cols(b, 2 * P)], in_=s_bank[pair, half][:, cols(b, 2 * P)],
+                                     func=ACT.Identity, scale=cf(1, cb), bias=cf(0, cb))
+
+        def s_product(pair, half):
+            dst = pair_tile(p1, "p1", pair, half)
+            nc.vector.tensor_tensor(out=dst.rearrange("p b r -> p (b r)"), in0=s_bank[pair, half][:], in1=lin_a[pair, half][:], op=ALU.mult)
+
+        def piece(store, rb, cb):
+            return store[rb // 2][:, cb, cols(rb % 2, P)]
+
+        am, sq, t_bank, c6t, p2, q_bank, b0_bank, q_row = {}, {}, {}, {}, {}, {}, {}, {}
+
+        def a_matmul(rb, m, at):
+            am[rb, m] = bank_at(at)
+            for g in range(G):
+                mx(am[rb, m][:], e_q[m, rb], cols(g, P), u_q[g], cols(0, C), g)
+
+        def square(rb, m):
+            sq[rb, m] = work.tile([P, C], F32, name="sq%d" % m, tag="sq%d" % m)
+            nc.scalar.activation(out=sq[rb, m][:], in_=am[rb, m][:], func=ACT.Square, scale=3.0 ** -0.5)
+
+        def turn_add(bank, part, first, last):
+            for cb in range(CB):
+                nc.tensor.matmul(bank[:, cols(cb, P)], part(cb), ident[:], start=(first and cb == 0),
+                                 stop=(last and cb == CB - 1), is_transpose=True)
+
+        def t_turn(rb, m, at=None):
+            if m == 1:
+                t_bank[rb] = bank_at(at)
+            turn_add(t_bank[rb], lambda cb: sq[rb, m][:, cols(cb, P)], m == 1, m == M - 1)
+
+        def t_scale(rb):
+            c6t[rb] = work.tile([P, C], F32, name="c6t", tag="c6t")
+            for cb in range(CB):
+                if rb < TAILV:
+                    nc.scalar.activation(out=c6t[rb][:, cols(cb, P)], in_=t_bank[rb][:, cols(cb, P)], func=ACT.Copy, scale=cf(6, cb))
+                else:
+                    nc.vector.scalar_tensor_tensor(out=c6t[rb][:, cols(cb, P)], in0=t_bank[rb][:, cols(cb, P)], scalar=cf(6, cb),
+                                                   in1=piece(lin_q, rb, cb), op0=ALU.mult, op1=ALU.add)
+
+        def t_product(rb):
+            p2[rb] = work.tile([P, C], F32, name="p2", tag="p2")
+            nc.vector.tensor_tensor(out=p2[rb][:].rearrange("p (b r) -> p b r", b=CB),
+                                    in0=t_bank[rb][:].rearrange("p (b r) -> p b r", b=CB),
+                                    in1=lin_b[rb // 2][:, :, cols(rb % 2, P)], op=ALU.mult)
+
+        def q_open(rb, at):
+            q_bank[rb] = bank_at(at)
+            if rb < TAILV:
+                turn_add(q_bank[rb], lambda cb: piece(lin_q, rb, cb), True, False)
+
+        def q_close(rb):
+            turn_add(q_bank[rb], lambda cb: c6t[rb][:, cols(cb, P)], rb >= TAILV, True)
+
+        def b0_open(rb, at):
+            b0_bank[rb] = bank_at(at)
+            turn_add(b0_bank[rb], lambda cb: piece(p1, rb, cb), True, False)
+
+        def b0_close(rb):
+            turn_add(b0_bank[rb], lambda cb: p2[rb][:, cols(cb, P)], False, True)
+
+        def q_empty(rb):
+            q_row[rb] = work.tile([P, C], F32, name="q_row", tag="q_row")
+            nc.scalar.copy(out=q_row[rb][:], in_=q_bank[rb][:])
+
+        def b0_store(rb):
+            res = work.tile([P, C], F32, name="res0", tag="res0")
+            nc.scalar.copy(out=res[:], in_=b0_bank[rb][:])
+            nc.sync.dma_start(out=out[0, cols(rb, P), :], in_=res[:])
+
+        def b_store(rb, m):
+            res = work.tile([P, C], F32, name="res%d" % m, tag="res%d" % m)
+            nc.vector.tensor_tensor(out=res[:], in0=am[rb, m][:], in1=q_row[rb][:], op=ALU.mult)
+            nc.sync.dma_start(out=out[m, cols(rb, P), :], in_=res[:])
+
+        def turn_empty(m, rb, at=None):
+            e_turn(m, rb, at)
+            e_empty(m, rb)
+
+        def s_stage(pair, half, at):
+            s_matmul(pair, half, at)
+            s_linear(pair, half)
+            s_affine(lin_q, "lin_q", 4, 5, pair, half)
+            s_affine(lin_b, "lin_b", 2, 3, pair, half)
+
+        nc.vector.tensor_copy(out=coef_pad[0:J * CB, :], in_=coef_rows[:])
+        spread_scale(0)
+        spread_scale(1)
+        turn_coef()
+        w_interleave(0, nc.scalar.copy)
+        e_scale_up(1, 0)
+        e_scale_up(2, 0)
+        w_quant(0)
+        h_slab(0, 0)
+        h_slab(0, 1)
+        turn_empty(1, 0)
+        e_scale_up(3, 0)
+        h_quant(0, 0)
+        h_slab(0, 2)
+        h_slab(0, 3)
+        turn_empty(2, 0)
+        turn_empty(3, 0)
+        w_interleave(1, nc.vector.tensor_copy)
+        h_quant(0, 1)
+        e_scale_up(0, 0)
+        w_quant(1)
+        h_slab(1, 0)
+        h_slab(1, 1)
+        h_quant(1, 0)
+        h_slab(1, 2)
+        h_slab(1, 3)
+        turn_empty(0, 0)
+        e_scale_up(0, 1)
+        h_quant(1, 1)
+        e_scale_up(1, 1)
+        for cb in range(CB):
+            u_block(0, cb, bank_at(cb % 3))
+        turn_empty(0, 1)
+        e_scale_up(2, 1)
+        e_quant(1, 0)
+        e_quant(2, 0)
+        e_quant(3, 0)
+        e_scale_up(3, 1)
+        u_quant(0)
+        for cb in range(CB):
+            u_block(1, cb, bank_at((cb + 1) % 3))
+        e_quant(0, 1)
+        e_scale_up(0, 2)
+        u_quant(1)
+        e_scale_up(0, 3)
+        turn_empty(1, 1, 3)
+        turn_empty(2, 1, 4)
+        turn_empty(3, 1, 5)
+        s_stage(0, 0, 3)
+        turn_empty(0, 2, 6)
+        turn_empty(0, 3, 4)
+        s_stage(0, 1, 7)
+        e_scale_up(0, 4)
+        e_scale_up(1, 2)
+        s_product(0, 0)
+        e_scale_up(2, 2)
+        e_quant(0, 3)
+        s_product(0, 1)
+
+        for rb in range(RB - 2):
+            pair, half = rb // 2 + 1, rb % 2
+            has_unit = rb + 4 < RB
+            for m in range(1, M):
+                a_matmul(rb, m, m - 1)
+                square(rb, m)
+            s_matmul(pair, half, 3)
+            if rb > 0:
+                e_scale_up(2, rb + 2)
+            e_quant(1, rb + 1)
+            e_scale_up(3, rb + 2)
+            e_quant(2, rb + 1)
+            if rb + 5 < RB:
+                e_scale_up(0, rb + 5)
+            if has_unit:
+                turn_empty(0, rb + 4, 5)
+            else:
+                s_linear(pair, half)
+            t_turn(rb, 1, 4)
+            q_open(rb, 6)
+            t_turn(rb, 2)
+            t_turn(rb, 3)
+            b0_open(rb, 5)
+            e_turn(1, rb + 2, 7)
+            t_scale(rb)
+            t_product(rb)
+            if has_unit:
+                s_linear(pair, half)
+                s_product(pair, half)
+            else:
+                s_affine(lin_q, "lin_q", 4, 5, pair, half)
+            e_quant(3, rb + 1)
+            q_close(rb)
+            q_empty(rb)
+            b0_close(rb)
+            if has_unit:
+                s_affine(lin_q, "lin_q", 4, 5, pair, half)
+                s_affine(lin_b, "lin_b", 2, 3, pair, half)
+                b0_store(rb)
+            for m in range(1, M):
+                b_store(rb, m)
+            e_empty(1, rb + 2)
+            turn_empty(2, rb + 2, 4)
+            if has_unit:
+                e_quant(0, rb + 4)
+            else:
+                b0_store(rb)
+            turn_empty(3, rb + 2, 6)
+            if not has_unit:
+                s_affine(lin_b, "lin_b", 2, 3, pair, half)
+                if rb + 3 == RB:
+                    for m in range(1, M):
+                        e_quant(m, rb + 2)
+                s_product(pair, half)
+            if rb + 3 < RB:
+                e_scale_up(1, rb + 3)
+
+        ra, rz = RB - 2, RB - 1
+        for m in range(1, M):
+            a_matmul(ra, m, m - 1)
+            square(ra, m)
+        a_matmul(rz, 1, 7)
+        a_matmul(rz, 2, 4)
+        a_matmul(rz, 3, 6)
+        for m in range(1, M):
+            t_turn(ra, m, 5)
+        for m in range(1, M):
+            square(rz, m)
+        t_scale(ra)
+        t_product(ra)
+        t_turn(rz, 1, 3)
+        t_turn(rz, 2)
+        q_open(ra, 5)
+        q_close(ra)
+        t_turn(rz, 3)
+        q_empty(ra)
+        t_scale(rz)
+        t_product(rz)
+        b0_open(ra, 5)
+        q_open(rz, 3)
+        q_close(rz)
+        b0_close(ra)
+        q_empty(rz)
+        b0_store(ra)
+        for m in range(1, M):
+            b_store(ra, m)
+        b0_open(rz, 0)
+        b0_close(rz)
+        b0_store(rz)
+        for m in range(1, M):
+            b_store(rz, m)

@@ -21,6 +21,10 @@ KP = 512
 CB = C // P
 RB = R // P
 TAILV = 6
+EV = 9
+LB = 0
+LBF = 1
+LH = 0
 
 
 def tile_macedensitytricksymmetriccontraction_kernel(tc, h, w, e_bytes, e_scale, coef, out):
@@ -67,11 +71,11 @@ def tile_macedensitytricksymmetriccontraction_kernel(tc, h, w, e_bytes, e_scale,
 
         load_w(0)
         load_ea(0)
+        load_w(1)
         load_h(0, 0)
         load_h(0, 1)
-        load_w(1)
-        load_h(1, 0)
         load_es(0)
+        load_h(1, 0)
         load_h(1, 1)
         load_ea(1)
         load_es(1)
@@ -89,12 +93,12 @@ def tile_macedensitytricksymmetriccontraction_kernel(tc, h, w, e_bytes, e_scale,
         scale_row = keep.tile([P, N], F32, name="scale_row")
         coef_col = keep.tile([P, J * CB], F32, name="coef_col")
 
-        def spread_scale(g):
+        def spread_scale(g, copy):
             bank = rot_bank()
             for t in range(4):
                 nc.tensor.transpose(bank[:, t * P:(t + 1) * P], scale_col[:, g, t:t + 1].to_broadcast([P, P]), ident[:])
-            nc.vector.tensor_copy(out=scale_row[:, g * KP:(g + 1) * KP].rearrange("q (p t) -> q p t", t=4),
-                                  in_=bank[:].rearrange("q (t p) -> q p t", t=4))
+            copy(out=scale_row[:, g * KP:(g + 1) * KP].rearrange("q (p t) -> q p t", t=4),
+                 in_=bank[:].rearrange("q (t p) -> q p t", t=4))
 
         def turn_coef():
             bank = rot_bank()
@@ -166,7 +170,7 @@ def tile_macedensitytricksymmetriccontraction_kernel(tc, h, w, e_bytes, e_scale,
 
         def e_scale_up(m, rb):
             src = es_bytes[rb // 2][:, rb % 2, :] if m == 0 else ea_bytes[rb][:, m - 1, :]
-            e_val[m, rb] = work.tile([P, N], BF16, name="e_val", tag="e_val", bufs=6)
+            e_val[m, rb] = work.tile([P, N], BF16, name="e_val", tag="e_val", bufs=EV)
             nc.vector.tensor_tensor(out=e_val[m, rb][:], in0=src.bitcast(FP8), in1=scale_row[:], op=ALU.mult)
 
         def e_turn(m, rb, at=None):
@@ -203,17 +207,23 @@ def tile_macedensitytricksymmetriccontraction_kernel(tc, h, w, e_bytes, e_scale,
                 store[pair] = work.tile([P, CB, 2 * P], F32, name=name, tag=name)
             return store[pair][:, 2 * half:2 * half + 2, :]
 
-        def s_affine(store, name, j0, j1, pair, half):
-            dst = pair_tile(store, name, pair, half)
-            for b in range(2):
+        def s_affine(store, name, j0, j1, pair, half, blocks=(0, 1), on_vector=False):
+            for b in blocks:
                 cb = 2 * half + b
-                nc.scalar.activation(out=dst[:, b, :], in_=s_bank[pair, half][:, cols(b, 2 * P)],
-                                     func=ACT.Identity, scale=cf(j1, cb), bias=cf(j0, cb))
+                if cb == 0:
+                    store[pair] = work.tile([P, CB, 2 * P], F32, name=name, tag=name)
+                if on_vector:
+                    nc.vector.tensor_scalar(out=store[pair][:, cb, :], in0=s_bank[pair, half][:, cols(b, 2 * P)],
+                                            scalar1=cf(j1, cb), scalar2=cf(j0, cb), op0=ALU.mult, op1=ALU.add)
+                else:
+                    nc.scalar.activation(out=store[pair][:, cb, :], in_=s_bank[pair, half][:, cols(b, 2 * P)],
+                                         func=ACT.Identity, scale=cf(j1, cb), bias=cf(j0, cb))
 
-        def s_linear(pair, half):
-            lin_a[pair, half] = work.tile([P, 512], F32, name="lin_a", tag="lin_a")
-            for b in range(2):
+        def s_linear(pair, half, blocks=(0, 1)):
+            for b in blocks:
                 cb = 2 * half + b
+                if b == 0:
+                    lin_a[pair, half] = work.tile([P, 512], F32, name="lin_a", tag="lin_a")
                 nc.scalar.activation(out=lin_a[pair, half][:, cols(b, 2 * P)], in_=s_bank[pair, half][:, cols(b, 2 * P)],
                                      func=ACT.Identity, scale=cf(1, cb), bias=cf(0, cb))
 
@@ -279,9 +289,9 @@ def tile_macedensitytricksymmetriccontraction_kernel(tc, h, w, e_bytes, e_scale,
             q_row[rb] = work.tile([P, C], F32, name="q_row", tag="q_row")
             nc.scalar.copy(out=q_row[rb][:], in_=q_bank[rb][:])
 
-        def b0_store(rb):
+        def b0_store(rb, copy=nc.scalar.copy):
             res = work.tile([P, C], F32, name="res0", tag="res0")
-            nc.scalar.copy(out=res[:], in_=b0_bank[rb][:])
+            copy(out=res[:], in_=b0_bank[rb][:])
             nc.sync.dma_start(out=out[0, cols(rb, P), :], in_=res[:])
 
         def b_store(rb, m):
@@ -297,66 +307,78 @@ def tile_macedensitytricksymmetriccontraction_kernel(tc, h, w, e_bytes, e_scale,
             s_matmul(pair, half, at)
             s_linear(pair, half)
             s_affine(lin_q, "lin_q", 4, 5, pair, half)
-            s_affine(lin_b, "lin_b", 2, 3, pair, half)
+            if LH <= half:
+                s_affine(lin_b, "lin_b", 2, 3, pair, half)
 
         nc.vector.tensor_copy(out=coef_pad[0:J * CB, :], in_=coef_rows[:])
-        spread_scale(0)
-        spread_scale(1)
+        spread_scale(0, nc.vector.tensor_copy)
+        spread_scale(1, nc.scalar.copy)
         turn_coef()
         w_interleave(0, nc.scalar.copy)
+        w_interleave(1, nc.scalar.copy)
         e_scale_up(1, 0)
         e_scale_up(2, 0)
+        e_scale_up(3, 0)
         w_quant(0)
         h_slab(0, 0)
         h_slab(0, 1)
-        turn_empty(1, 0)
-        e_scale_up(3, 0)
-        h_quant(0, 0)
         h_slab(0, 2)
         h_slab(0, 3)
-        turn_empty(2, 0)
-        turn_empty(3, 0)
-        w_interleave(1, nc.vector.tensor_copy)
-        h_quant(0, 1)
         e_scale_up(0, 0)
         w_quant(1)
+        h_quant(0, 0)
+        e_scale_up(0, 1)
+        h_quant(0, 1)
         h_slab(1, 0)
         h_slab(1, 1)
-        h_quant(1, 0)
         h_slab(1, 2)
         h_slab(1, 3)
-        turn_empty(0, 0)
-        e_scale_up(0, 1)
-        h_quant(1, 1)
         e_scale_up(1, 1)
+        h_quant(1, 0)
+        turn_empty(1, 0)
+        e_scale_up(2, 1)
+        h_quant(1, 1)
         for cb in range(CB):
             u_block(0, cb, bank_at(cb % 3))
-        turn_empty(0, 1)
-        e_scale_up(2, 1)
-        e_quant(1, 0)
-        e_quant(2, 0)
-        e_quant(3, 0)
+        turn_empty(2, 0)
+        turn_empty(3, 0)
         e_scale_up(3, 1)
+        e_scale_up(0, 2)
         u_quant(0)
         for cb in range(CB):
             u_block(1, cb, bank_at((cb + 1) % 3))
-        e_quant(0, 1)
-        e_scale_up(0, 2)
-        u_quant(1)
+        turn_empty(0, 0, 3)
+        turn_empty(0, 1, 4)
+        e_quant(1, 0)
+        e_quant(2, 0)
+        e_quant(3, 0)
         e_scale_up(0, 3)
-        turn_empty(1, 1, 3)
-        turn_empty(2, 1, 4)
-        turn_empty(3, 1, 5)
+        u_quant(1)
+        e_quant(0, 1)
+        turn_empty(1, 1, 5)
+        turn_empty(2, 1, 6)
+        turn_empty(3, 1, 7)
         s_stage(0, 0, 3)
         turn_empty(0, 2, 6)
         turn_empty(0, 3, 4)
         s_stage(0, 1, 7)
-        e_scale_up(0, 4)
-        e_scale_up(1, 2)
+        queue = [(m, rb + (4 if m == 0 else 2)) for rb in range(RB - 2) for m in range(M) if m > 0 or rb + 4 < RB]
+
+        def next_scale_up():
+            if queue:
+                e_scale_up(*queue.pop(0))
+
+        for n in range(3):
+            next_scale_up()
         s_product(0, 0)
-        e_scale_up(2, 2)
+        if LH > 0:
+            s_affine(lin_b, "lin_b", 2, 3, 0, 0, on_vector=True)
+        next_scale_up()
         e_quant(0, 3)
+        next_scale_up()
         s_product(0, 1)
+        if LH > 1:
+            s_affine(lin_b, "lin_b", 2, 3, 0, 1, on_vector=True)
 
         for rb in range(RB - 2):
             pair, half = rb // 2 + 1, rb % 2
@@ -365,17 +387,16 @@ def tile_macedensitytricksymmetriccontraction_kernel(tc, h, w, e_bytes, e_scale,
                 a_matmul(rb, m, m - 1)
                 square(rb, m)
             s_matmul(pair, half, 3)
-            if rb > 0:
-                e_scale_up(2, rb + 2)
             e_quant(1, rb + 1)
-            e_scale_up(3, rb + 2)
+            next_scale_up()
             e_quant(2, rb + 1)
-            if rb + 5 < RB:
-                e_scale_up(0, rb + 5)
+            next_scale_up()
             if has_unit:
                 turn_empty(0, rb + 4, 5)
+                s_linear(pair, half, (0,))
             else:
                 s_linear(pair, half)
+                s_affine(lin_q, "lin_q", 4, 5, pair, half, (0,))
             t_turn(rb, 1, 4)
             q_open(rb, 6)
             t_turn(rb, 2)
@@ -385,67 +406,74 @@ def tile_macedensitytricksymmetriccontraction_kernel(tc, h, w, e_bytes, e_scale,
             t_scale(rb)
             t_product(rb)
             if has_unit:
-                s_linear(pair, half)
-                s_product(pair, half)
+                s_linear(pair, half, (1,))
             else:
-                s_affine(lin_q, "lin_q", 4, 5, pair, half)
+                s_affine(lin_q, "lin_q", 4, 5, pair, half, (1,))
+            s_product(pair, half)
+            moved = LB if LBF <= rb < RB - 3 else 0
+            s_affine(lin_b, "lin_b", 2, 3, pair, half, (0, 1)[:moved], on_vector=True)
+            e_empty(1, rb + 2)
             e_quant(3, rb + 1)
             q_close(rb)
             q_empty(rb)
-            b0_close(rb)
-            if has_unit:
-                s_affine(lin_q, "lin_q", 4, 5, pair, half)
-                s_affine(lin_b, "lin_b", 2, 3, pair, half)
-                b0_store(rb)
-            for m in range(1, M):
-                b_store(rb, m)
-            e_empty(1, rb + 2)
-            turn_empty(2, rb + 2, 4)
-            if has_unit:
-                e_quant(0, rb + 4)
-            else:
-                b0_store(rb)
-            turn_empty(3, rb + 2, 6)
-            if not has_unit:
-                s_affine(lin_b, "lin_b", 2, 3, pair, half)
-                if rb + 3 == RB:
-                    for m in range(1, M):
-                        e_quant(m, rb + 2)
-                s_product(pair, half)
             if rb + 3 < RB:
-                e_scale_up(1, rb + 3)
+                b0_close(rb)
+                if has_unit:
+                    s_affine(lin_q, "lin_q", 4, 5, pair, half)
+                s_affine(lin_b, "lin_b", 2, 3, pair, half, (0, 1)[moved:])
+                b0_store(rb)
+                for m in range(1, M):
+                    b_store(rb, m)
+                turn_empty(2, rb + 2, 4)
+                turn_empty(3, rb + 2, 6)
+                if has_unit:
+                    e_quant(0, rb + 4)
+                next_scale_up()
+            else:
+                turn_empty(2, rb + 2, 4)
+                turn_empty(3, rb + 2, 6)
+                b0_close(rb)
+                e_quant(1, rb + 2)
+                b_store(rb, 1)
+                b_store(rb, 2)
+                e_quant(2, rb + 2)
+                b_store(rb, 3)
+                e_quant(3, rb + 2)
+                b0_store(rb, nc.vector.tensor_copy)
+                s_affine(lin_b, "lin_b", 2, 3, pair, half, on_vector=True)
 
         ra, rz = RB - 2, RB - 1
         for m in range(1, M):
             a_matmul(ra, m, m - 1)
             square(ra, m)
-        a_matmul(rz, 1, 7)
-        a_matmul(rz, 2, 4)
-        a_matmul(rz, 3, 6)
+        a_matmul(rz, 1, 4)
         for m in range(1, M):
-            t_turn(ra, m, 5)
+            t_turn(ra, m, 7)
+        a_matmul(rz, 2, 6)
+        a_matmul(rz, 3, 5)
         for m in range(1, M):
             square(rz, m)
         t_scale(ra)
         t_product(ra)
-        t_turn(rz, 1, 3)
-        t_turn(rz, 2)
-        q_open(ra, 5)
+        q_open(ra, 3)
         q_close(ra)
-        t_turn(rz, 3)
         q_empty(ra)
+        for m in range(1, M):
+            t_turn(rz, m, 7)
+        b_store(ra, 1)
+        b0_open(ra, 0)
+        b0_close(ra)
         t_scale(rz)
-        t_product(rz)
-        b0_open(ra, 5)
         q_open(rz, 3)
         q_close(rz)
-        b0_close(ra)
-        q_empty(rz)
+        b_store(ra, 2)
         b0_store(ra)
-        for m in range(1, M):
-            b_store(ra, m)
-        b0_open(rz, 0)
+        q_empty(rz)
+        t_product(rz)
+        b0_open(rz, 1)
         b0_close(rz)
+        b_store(ra, 3)
+        b_store(rz, 1)
         b0_store(rz)
-        for m in range(1, M):
-            b_store(rz, m)
+        b_store(rz, 2)
+        b_store(rz, 3)

@@ -16,15 +16,27 @@ ALU = mybir.AluOpType
 ACT = mybir.ActivationFunctionType
 
 P = 128
-G = 2
-KP = 512
+PACK = 4
+K_PASS = P * PACK
+G = N // K_PASS
+BANK = 512
 CB = C // P
 RB = R // P
-TAILV = 6
-EV = 9
-LB = 0
-LBF = 1
-LH = 0
+VEC = range(1, M)
+
+S_BANK = 3
+T_THEN_UNIT = 4
+UNIT_THEN_B0 = 5
+Q_THEN_UNIT = 6
+UNIT_BANK = 7
+SPARE = (3, 4, 5, 6, 7)
+
+A_AHEAD = 2
+S_AHEAD = 4
+SCALED_BUFS = 9
+TURNED_BUFS = 6
+CODE_BUFS = 9
+EXTRA_SCALE_AT = 1
 
 
 def tile_macedensitytricksymmetriccontraction_kernel(tc, h, w, e_bytes, e_scale, coef, out):
@@ -35,81 +47,78 @@ def tile_macedensitytricksymmetriccontraction_kernel(tc, h, w, e_bytes, e_scale,
         psum = ctx.enter_context(tc.psum_pool(name="psum", bufs=1))
         ctx.enter_context(tc.manual_schedule())
 
-        turns = []
+        def cols(i, n):
+            return slice(i * n, (i + 1) * n)
 
         def bank_at(i):
-            return psum.tile([P, 512], F32, name="bank%d" % i, tag="bank%d" % i)
+            return psum.tile([P, BANK], F32, name="bank%d" % i, tag="bank%d" % i)
 
-        def rot_bank():
-            turns.append(None)
-            return bank_at(3 + len(turns) % 5)
+        spare_taken = []
 
-        scale_col = keep.tile([P, G, 4], F32, name="scale_col")
-        nc.sync.dma_start(out=scale_col[:], in_=e_scale[0, 0, :].rearrange("(g p t) -> p g t", g=G, t=4))
+        def spare_bank():
+            spare_taken.append(None)
+            return bank_at(SPARE[len(spare_taken) % len(SPARE)])
+
+        scale_col = keep.tile([P, G, PACK], F32, name="scale_col")
+        nc.sync.dma_start(out=scale_col[:], in_=e_scale[0, 0, :].rearrange("(g p t) -> p g t", g=G, t=PACK))
         coef_rows = keep.tile([J * CB, P], BF16, name="coef_rows")
         nc.sync.dma_start(out=coef_rows[:], in_=coef.rearrange("j (b p) -> (j b) p", p=P))
 
-        w_raw, h_raw, ea_bytes, es_bytes = {}, {}, {}, {}
+        w_raw, h_raw, vec_bytes, s_bytes = {}, {}, {}, {}
 
         def load_w(g):
-            w_raw[g] = keep.tile([P, 4, C], BF16, name="w_raw%d" % g)
-            nc.sync.dma_start(out=w_raw[g][:], in_=w[g * KP:(g + 1) * KP, :].rearrange("(p t) c -> p t c", t=4))
+            w_raw[g] = keep.tile([P, PACK, C], BF16, name="w_raw%d" % g)
+            nc.sync.dma_start(out=w_raw[g][:], in_=w[cols(g, K_PASS), :].rearrange("(p t) c -> p t c", t=PACK))
 
         def load_h(g, half):
             h_raw[g, half] = keep.tile([P, 2 * D], BF16, name="h_raw%d_%d" % (g, half))
-            rows = h[g * KP:(g + 1) * KP, :].rearrange("(p s t) d -> p s (t d)", s=2, t=2)
+            rows = h[cols(g, K_PASS), :].rearrange("(p s t) d -> p s (t d)", s=2, t=2)
             nc.sync.dma_start(out=h_raw[g, half][:], in_=rows[:, half, :])
 
-        def load_ea(rb):
-            ea_bytes[rb] = keep.tile([P, M - 1, N], U8, name="ea_bytes%d" % rb)
-            nc.sync.dma_start(out=ea_bytes[rb][:], in_=e_bytes[1:M, rb * P:(rb + 1) * P, :].rearrange("m r k -> r m k"))
+        def load_vec_bytes(rb):
+            vec_bytes[rb] = keep.tile([P, M - 1, N], U8, name="vec_bytes%d" % rb)
+            nc.sync.dma_start(out=vec_bytes[rb][:], in_=e_bytes[1:M, cols(rb, P), :].rearrange("m r k -> r m k"))
 
-        def load_es(pair):
-            es_bytes[pair] = keep.tile([P, 2, N], U8, name="es_bytes%d" % pair)
-            nc.sync.dma_start(out=es_bytes[pair][:],
-                              in_=e_bytes[0, pair * 2 * P:(pair + 1) * 2 * P, :].rearrange("(b r) k -> r b k", b=2))
+        def load_s_bytes(pair):
+            s_bytes[pair] = keep.tile([P, 2, N], U8, name="s_bytes%d" % pair)
+            nc.sync.dma_start(out=s_bytes[pair][:], in_=e_bytes[0, cols(pair, 2 * P), :].rearrange("(b r) k -> r b k", b=2))
 
         load_w(0)
-        load_ea(0)
-        load_w(1)
+        load_vec_bytes(0)
         load_h(0, 0)
         load_h(0, 1)
-        load_es(0)
+        load_w(1)
         load_h(1, 0)
+        load_s_bytes(0)
         load_h(1, 1)
-        load_ea(1)
-        load_es(1)
-        for rb in range(2, RB):
-            load_ea(rb)
-            if rb < 4:
-                load_es(rb)
+        for rb in range(1, RB):
+            load_vec_bytes(rb)
+            if rb < RB // 2:
+                load_s_bytes(rb)
 
         ident = keep.tile([P, P], F32, name="ident")
         make_identity(nc, ident[:])
         coef_pad = keep.tile([P, P], F32, name="coef_pad")
-        nc.vector.memset(coef_pad[:], 0.0)
-        warm = keep.tile([P, 1], F32, name="warm")
-        nc.scalar.activation(out=warm[:], in_=coef_pad[:, 0:1], func=ACT.Square)
         scale_row = keep.tile([P, N], F32, name="scale_row")
         coef_col = keep.tile([P, J * CB], F32, name="coef_col")
 
-        def spread_scale(g, copy):
-            bank = rot_bank()
-            for t in range(4):
-                nc.tensor.transpose(bank[:, t * P:(t + 1) * P], scale_col[:, g, t:t + 1].to_broadcast([P, P]), ident[:])
-            copy(out=scale_row[:, g * KP:(g + 1) * KP].rearrange("q (p t) -> q p t", t=4),
-                 in_=bank[:].rearrange("q (t p) -> q p t", t=4))
+        def spread_scale(g):
+            bank = spare_bank()
+            for t in range(PACK):
+                nc.tensor.transpose(bank[:, cols(t, P)], scale_col[:, g, t:t + 1].to_broadcast([P, P]), ident[:])
+            nc.vector.tensor_copy(out=scale_row[:, cols(g, K_PASS)].rearrange("q (p t) -> q p t", t=PACK),
+                                  in_=bank[:].rearrange("q (t p) -> q p t", t=PACK))
 
         def turn_coef():
-            bank = rot_bank()
-            nc.tensor.transpose(bank[:, 0:P], coef_pad[:], ident[:])
+            bank = spare_bank()
+            nc.tensor.matmul(bank[:, 0:P], coef_pad[:], ident[:], start=True, stop=True, is_transpose=False)
             nc.vector.tensor_copy(out=coef_col[:], in_=bank[:, 0:J * CB])
 
         def cf(j, cb):
             return coef_col[:, j * CB + cb:j * CB + cb + 1]
 
         def quantize(name, src, bufs=1):
-            width = src.shape[1] // 4
+            width = src.shape[1] // PACK
             codes = keep.tile([P, width], U32, name=name + "_codes", tag=name + "_codes", bufs=bufs, align_bytes=64)
             scales = keep.tile([P, width], U8, name=name + "_scales", tag=name + "_scales", bufs=bufs, align_bytes=64)
             nc.vector.quantize_mx(out=codes[:].bitcast(FP8X4), scales=scales[:], in_=src)
@@ -120,170 +129,176 @@ def tile_macedensitytricksymmetriccontraction_kernel(tc, h, w, e_bytes, e_scale,
                                 rhs=rhs[0][:, rcols].bitcast(FP8X4), rhs_scale=rhs[1][:, rcols],
                                 start=(g == 0), stop=(g == G - 1))
 
-        def cols(i, n):
-            return slice(i * n, (i + 1) * n)
-
         def turn_rows(rows, bank):
             words = rows.bitcast(F32)
             for g in range(G):
                 for u in range(2):
-                    nc.tensor.transpose(bank[:, cols(2 * g + u, P)], words[:, 256 * g + u:256 * (g + 1):2], ident[:])
+                    nc.tensor.transpose(bank[:, cols(2 * g + u, P)], words[:, 2 * P * g + u:2 * P * (g + 1):2], ident[:])
             return bank
+
+        def as_words(tile):
+            return tile.bitcast(F32).rearrange("p (g r u) -> p g r u", g=G, u=2)
 
         def empty_turned(bank, dst_words):
             nc.scalar.copy(out=dst_words, in_=bank[:].rearrange("p (g u r) -> p g r u", g=G, u=2))
 
-        w_in, w_q, h_in, h_q, h_bank, u_in, u_q, u_bank = {}, {}, {}, {}, {}, {}, {}, {}
+        w_in, w_q, h_in, h_q, u_in, u_q = {}, {}, {}, {}, {}, {}
 
         def w_interleave(g, copy):
-            w_in[g] = keep.tile([P, 4 * C], BF16, name="w_in%d" % g, tag="wu_in%d" % g, align_bytes=64)
-            copy(out=w_in[g][:].rearrange("p (c i t) -> p c t i", i=4, t=4),
+            w_in[g] = keep.tile([P, PACK * C], BF16, name="w_in%d" % g, tag="wu_in%d" % g, align_bytes=64)
+            copy(out=w_in[g][:].rearrange("p (c i t) -> p c t i", i=4, t=PACK),
                  in_=w_raw[g][:].rearrange("p t (c i) -> p c t i", i=4))
 
         def w_quant(g):
             w_q[g] = quantize("w%d" % g, w_in[g][:])
 
         def h_slab(g, t):
-            half = t // 2
             if t % 2 == 0:
-                h_in[g, half] = keep.tile([P, 2 * D], BF16, name="h_in%d_%d" % (g, half), align_bytes=64)
-            bank = turn_rows(h_raw[g, half][:, cols(t % 2, D)], rot_bank())
-            dst = h_in[g, half][:, cols(t % 2, D)].bitcast(F32).rearrange("p (g r u) -> p g r u", g=G, u=2)
-            empty_turned(bank, dst)
+                h_in[g, t // 2] = keep.tile([P, 2 * D], BF16, name="h_in%d_%d" % (g, t // 2), align_bytes=64)
+            bank = turn_rows(h_raw[g, t // 2][:, cols(t % 2, D)], spare_bank())
+            empty_turned(bank, as_words(h_in[g, t // 2][:, cols(t % 2, D)]))
 
         def h_quant(g, half):
             h_q[g, half] = quantize("h%d_%d" % (g, half), h_in[g, half][:])
 
-        def u_block(g, cb, bank):
+        def u_block(g, cb):
+            bank = bank_at((g * CB + cb) % 3)
             if cb == 0:
-                u_in[g] = keep.tile([P, 4 * C], BF16, name="u_in%d" % g, tag="wu_in%d" % g, align_bytes=64)
-            for t in range(4):
+                u_in[g] = keep.tile([P, PACK * C], BF16, name="u_in%d" % g, tag="wu_in%d" % g, align_bytes=64)
+            for t in range(PACK):
                 for dg in range(G):
                     mx(bank[:, cols(t, P)], h_q[g, t // 2], cols((t % 2) * G + dg, P), w_q[dg], cols(cb, P), dg)
-            nc.scalar.copy(out=u_in[g][:, cols(cb, 4 * P)].rearrange("p (c t) -> p c t", t=4),
-                           in_=bank[:].rearrange("p (t c) -> p c t", t=4))
+            nc.scalar.copy(out=u_in[g][:, cols(cb, PACK * P)].rearrange("p (c t) -> p c t", t=PACK),
+                           in_=bank[:].rearrange("p (t c) -> p c t", t=PACK))
 
         def u_quant(g):
             u_q[g] = quantize("u%d" % g, u_in[g][:])
 
-        e_val, e_bank, e_in, e_q = {}, {}, {}, {}
+        e_val, e_bank, e_in, vec_q, s_q = {}, {}, {}, {}, {}
 
         def e_scale_up(m, rb):
-            src = es_bytes[rb // 2][:, rb % 2, :] if m == 0 else ea_bytes[rb][:, m - 1, :]
-            e_val[m, rb] = work.tile([P, N], BF16, name="e_val", tag="e_val", bufs=EV)
+            src = s_bytes[rb // 2][:, rb % 2, :] if m == 0 else vec_bytes[rb][:, m - 1, :]
+            e_val[m, rb] = work.tile([P, N], BF16, name="e_val", tag="e_val", bufs=SCALED_BUFS)
             nc.vector.tensor_tensor(out=e_val[m, rb][:], in0=src.bitcast(FP8), in1=scale_row[:], op=ALU.mult)
 
-        def e_turn(m, rb, at=None):
-            e_bank[m, rb] = turn_rows(e_val[m, rb][:], rot_bank() if at is None else bank_at(at))
+        def e_turn(m, rb, bank):
+            e_bank[m, rb] = turn_rows(e_val[m, rb][:], bank)
 
         def e_empty(m, rb):
             if m == 0:
                 if rb % 2 == 0:
-                    e_in[0, rb // 2] = work.tile([P, 2 * N], BF16, name="es_in", tag="es_in", bufs=2, align_bytes=64)
-                words = e_in[0, rb // 2][:].bitcast(F32).rearrange("p (g r u) -> p g r u", g=G, u=2)
-                dst = words[:, :, cols(rb % 2, P), :]
+                    e_in[0, rb // 2] = work.tile([P, 2 * N], BF16, name="s_in", tag="s_in", align_bytes=64)
+                dst = as_words(e_in[0, rb // 2][:])[:, :, cols(rb % 2, P), :]
             else:
-                e_in[m, rb] = work.tile([P, N], BF16, name="ea_in", tag="ea_in", bufs=6, align_bytes=64)
-                dst = e_in[m, rb][:].bitcast(F32).rearrange("p (g r u) -> p g r u", g=G, u=2)
+                e_in[m, rb] = work.tile([P, N], BF16, name="vec_in", tag="vec_in", bufs=TURNED_BUFS, align_bytes=64)
+                dst = as_words(e_in[m, rb][:])
             empty_turned(e_bank[m, rb], dst)
 
-        def e_quant(m, rb):
-            if m == 0:
-                if rb % 2 == 1:
-                    e_q[0, rb // 2] = quantize("es", e_in[0, rb // 2][:], 2)
-            else:
-                e_q[m, rb] = quantize("ea", e_in[m, rb][:], 9)
+        def turn_empty(m, rb, bank):
+            e_turn(m, rb, bank)
+            e_empty(m, rb)
 
-        s_bank, lin_a, lin_b, lin_q, p1 = {}, {}, {}, {}, {}
+        def vec_quant(m, rb):
+            vec_q[m, rb] = quantize("vec", e_in[m, rb][:], CODE_BUFS)
+
+        def s_quant(pair):
+            s_q[pair] = quantize("s", e_in[0, pair][:], 2)
+
+        s_bank, lin_s, lin_t, lin_q, prod_s = {}, {}, {}, {}, {}
 
         def s_matmul(pair, half, at):
-            bank = s_bank[pair, half] = bank_at(at)
+            s_bank[pair, half] = bank_at(at)
             for b in range(2):
                 for g in range(G):
-                    mx(bank[:, cols(b, 2 * P)], u_q[g], cols(2 * half + b, P), e_q[0, pair], cols(g, 2 * P), g)
+                    mx(s_bank[pair, half][:, cols(b, 2 * P)], u_q[g], cols(2 * half + b, P), s_q[pair], cols(g, 2 * P), g)
 
-        def pair_tile(store, name, pair, half):
-            if half == 0:
+        def affine(dst, j, pair, half, b, on_vector):
+            src, cb = s_bank[pair, half][:, cols(b, 2 * P)], 2 * half + b
+            if on_vector:
+                nc.vector.tensor_scalar(out=dst, in0=src, scalar1=cf(j + 1, cb), scalar2=cf(j, cb), op0=ALU.mult, op1=ALU.add)
+            else:
+                nc.scalar.activation(out=dst, in_=src, func=ACT.Identity, scale=cf(j + 1, cb), bias=cf(j, cb))
+
+        def pair_block(store, name, pair, cb):
+            if cb == 0:
                 store[pair] = work.tile([P, CB, 2 * P], F32, name=name, tag=name)
-            return store[pair][:, 2 * half:2 * half + 2, :]
+            return store[pair][:, cb, :]
 
-        def s_affine(store, name, j0, j1, pair, half, blocks=(0, 1), on_vector=False):
+        def make_lin_s(pair, half, blocks=(0, 1)):
             for b in blocks:
-                cb = 2 * half + b
-                if cb == 0:
-                    store[pair] = work.tile([P, CB, 2 * P], F32, name=name, tag=name)
-                if on_vector:
-                    nc.vector.tensor_scalar(out=store[pair][:, cb, :], in0=s_bank[pair, half][:, cols(b, 2 * P)],
-                                            scalar1=cf(j1, cb), scalar2=cf(j0, cb), op0=ALU.mult, op1=ALU.add)
-                else:
-                    nc.scalar.activation(out=store[pair][:, cb, :], in_=s_bank[pair, half][:, cols(b, 2 * P)],
-                                         func=ACT.Identity, scale=cf(j1, cb), bias=cf(j0, cb))
-
-        def s_linear(pair, half, blocks=(0, 1)):
-            for b in blocks:
-                cb = 2 * half + b
                 if b == 0:
-                    lin_a[pair, half] = work.tile([P, 512], F32, name="lin_a", tag="lin_a")
-                nc.scalar.activation(out=lin_a[pair, half][:, cols(b, 2 * P)], in_=s_bank[pair, half][:, cols(b, 2 * P)],
-                                     func=ACT.Identity, scale=cf(1, cb), bias=cf(0, cb))
+                    lin_s[pair, half] = work.tile([P, BANK], F32, name="lin_s", tag="lin_s")
+                affine(lin_s[pair, half][:, cols(b, 2 * P)], 0, pair, half, b, False)
 
-        def s_product(pair, half):
-            dst = pair_tile(p1, "p1", pair, half)
-            nc.vector.tensor_tensor(out=dst.rearrange("p b r -> p (b r)"), in0=s_bank[pair, half][:], in1=lin_a[pair, half][:], op=ALU.mult)
+        def make_lin_t(pair, half, on_vector=False):
+            for b in range(2):
+                affine(pair_block(lin_t, "lin_t", pair, 2 * half + b), 2, pair, half, b, on_vector)
+
+        def make_lin_q(pair, half, blocks=(0, 1)):
+            for b in blocks:
+                affine(pair_block(lin_q, "lin_q", pair, 2 * half + b), 4, pair, half, b, False)
+
+        def make_prod_s(pair, half):
+            if half == 0:
+                prod_s[pair] = work.tile([P, CB, 2 * P], F32, name="prod_s", tag="prod_s")
+            dst = prod_s[pair][:, cols(half, 2), :].rearrange("p b r -> p (b r)")
+            nc.vector.tensor_tensor(out=dst, in0=s_bank[pair, half][:], in1=lin_s[pair, half][:], op=ALU.mult)
 
         def piece(store, rb, cb):
             return store[rb // 2][:, cb, cols(rb % 2, P)]
 
-        am, sq, t_bank, c6t, p2, q_bank, b0_bank, q_row = {}, {}, {}, {}, {}, {}, {}, {}
+        am, sq, t_bank, q_term, prod_t, q_bank, b0_bank, q_row = {}, {}, {}, {}, {}, {}, {}, {}
 
         def a_matmul(rb, m, at):
             am[rb, m] = bank_at(at)
             for g in range(G):
-                mx(am[rb, m][:], e_q[m, rb], cols(g, P), u_q[g], cols(0, C), g)
+                mx(am[rb, m][:], vec_q[m, rb], cols(g, P), u_q[g], cols(0, C), g)
 
         def square(rb, m):
             sq[rb, m] = work.tile([P, C], F32, name="sq%d" % m, tag="sq%d" % m)
             nc.scalar.activation(out=sq[rb, m][:], in_=am[rb, m][:], func=ACT.Square, scale=3.0 ** -0.5)
 
-        def turn_add(bank, part, first, last):
-            for cb in range(CB):
+        def turn_add(bank, part, first, last, blocks=range(CB), plain=False):
+            for cb in blocks:
                 nc.tensor.matmul(bank[:, cols(cb, P)], part(cb), ident[:], start=(first and cb == 0),
-                                 stop=(last and cb == CB - 1), is_transpose=True)
+                                 stop=(last and cb == CB - 1), is_transpose=(not plain))
 
-        def t_turn(rb, m, at=None):
+        def t_turn(rb, m, at):
             if m == 1:
                 t_bank[rb] = bank_at(at)
             turn_add(t_bank[rb], lambda cb: sq[rb, m][:, cols(cb, P)], m == 1, m == M - 1)
 
-        def t_scale(rb):
-            c6t[rb] = work.tile([P, C], F32, name="c6t", tag="c6t")
+        def make_c6t(rb):
+            q_term[rb] = work.tile([P, C], F32, name="q_term", tag="q_term")
             for cb in range(CB):
-                if rb < TAILV:
-                    nc.scalar.activation(out=c6t[rb][:, cols(cb, P)], in_=t_bank[rb][:, cols(cb, P)], func=ACT.Copy, scale=cf(6, cb))
-                else:
-                    nc.vector.scalar_tensor_tensor(out=c6t[rb][:, cols(cb, P)], in0=t_bank[rb][:, cols(cb, P)], scalar=cf(6, cb),
-                                                   in1=piece(lin_q, rb, cb), op0=ALU.mult, op1=ALU.add)
+                nc.scalar.activation(out=q_term[rb][:, cols(cb, P)], in_=t_bank[rb][:, cols(cb, P)], func=ACT.Copy, scale=cf(6, cb))
 
-        def t_product(rb):
-            p2[rb] = work.tile([P, C], F32, name="p2", tag="p2")
-            nc.vector.tensor_tensor(out=p2[rb][:].rearrange("p (b r) -> p b r", b=CB),
+        def make_whole_q(rb):
+            q_term[rb] = work.tile([P, C], F32, name="q_term", tag="q_term")
+            for cb in range(CB):
+                nc.vector.scalar_tensor_tensor(out=q_term[rb][:, cols(cb, P)], in0=t_bank[rb][:, cols(cb, P)], scalar=cf(6, cb),
+                                               in1=piece(lin_q, rb, cb), op0=ALU.mult, op1=ALU.add)
+
+        def make_prod_t(rb):
+            prod_t[rb] = work.tile([P, C], F32, name="prod_t", tag="prod_t")
+            nc.vector.tensor_tensor(out=prod_t[rb][:].rearrange("p (b r) -> p b r", b=CB),
                                     in0=t_bank[rb][:].rearrange("p (b r) -> p b r", b=CB),
-                                    in1=lin_b[rb // 2][:, :, cols(rb % 2, P)], op=ALU.mult)
+                                    in1=lin_t[rb // 2][:, :, cols(rb % 2, P)], op=ALU.mult)
 
         def q_open(rb, at):
             q_bank[rb] = bank_at(at)
-            if rb < TAILV:
-                turn_add(q_bank[rb], lambda cb: piece(lin_q, rb, cb), True, False)
+            turn_add(q_bank[rb], lambda cb: piece(lin_q, rb, cb), True, False)
 
-        def q_close(rb):
-            turn_add(q_bank[rb], lambda cb: c6t[rb][:, cols(cb, P)], rb >= TAILV, True)
+        def q_close(rb, opens=False):
+            turn_add(q_bank[rb], lambda cb: q_term[rb][:, cols(cb, P)], opens, True)
 
-        def b0_open(rb, at):
-            b0_bank[rb] = bank_at(at)
-            turn_add(b0_bank[rb], lambda cb: piece(p1, rb, cb), True, False)
+        def b0_open(rb, at, blocks=range(CB), plain=False):
+            if 0 in blocks:
+                b0_bank[rb] = bank_at(at)
+            turn_add(b0_bank[rb], lambda cb: piece(prod_s, rb, cb), True, False, blocks, plain)
 
         def b0_close(rb):
-            turn_add(b0_bank[rb], lambda cb: p2[rb][:, cols(cb, P)], False, True)
+            turn_add(b0_bank[rb], lambda cb: prod_t[rb][:, cols(cb, P)], False, True)
 
         def q_empty(rb):
             q_row[rb] = work.tile([P, C], F32, name="q_row", tag="q_row")
@@ -299,181 +314,176 @@ def tile_macedensitytricksymmetriccontraction_kernel(tc, h, w, e_bytes, e_scale,
             nc.vector.tensor_tensor(out=res[:], in0=am[rb, m][:], in1=q_row[rb][:], op=ALU.mult)
             nc.sync.dma_start(out=out[m, cols(rb, P), :], in_=res[:])
 
-        def turn_empty(m, rb, at=None):
-            e_turn(m, rb, at)
-            e_empty(m, rb)
-
-        def s_stage(pair, half, at):
-            s_matmul(pair, half, at)
-            s_linear(pair, half)
-            s_affine(lin_q, "lin_q", 4, 5, pair, half)
-            if LH <= half:
-                s_affine(lin_b, "lin_b", 2, 3, pair, half)
-
-        nc.vector.tensor_copy(out=coef_pad[0:J * CB, :], in_=coef_rows[:])
-        spread_scale(0, nc.vector.tensor_copy)
-        spread_scale(1, nc.scalar.copy)
-        turn_coef()
+        nc.vector.memset(coef_pad[:], 0.0)
+        nc.scalar.activation(out=coef_pad[0:J * CB, :], in_=coef_rows[:], func=ACT.Identity)
+        spread_scale(0)
+        spread_scale(1)
         w_interleave(0, nc.scalar.copy)
-        w_interleave(1, nc.scalar.copy)
-        e_scale_up(1, 0)
-        e_scale_up(2, 0)
-        e_scale_up(3, 0)
+        for m in VEC:
+            e_scale_up(m, 0)
         w_quant(0)
-        h_slab(0, 0)
-        h_slab(0, 1)
-        h_slab(0, 2)
-        h_slab(0, 3)
-        e_scale_up(0, 0)
-        w_quant(1)
+        turn_empty(1, 0, spare_bank())
+        for t in range(PACK):
+            h_slab(0, t)
         h_quant(0, 0)
-        e_scale_up(0, 1)
+        w_interleave(1, nc.vector.tensor_copy)
         h_quant(0, 1)
+        w_quant(1)
+        e_scale_up(0, 0)
+        turn_empty(2, 0, spare_bank())
         h_slab(1, 0)
+        turn_coef()
         h_slab(1, 1)
+        turn_empty(3, 0, spare_bank())
+        e_scale_up(0, 1)
+        h_quant(1, 0)
+        u_block(0, 0)
+        u_block(0, 1)
         h_slab(1, 2)
         h_slab(1, 3)
         e_scale_up(1, 1)
-        h_quant(1, 0)
-        turn_empty(1, 0)
-        e_scale_up(2, 1)
+        vec_quant(1, 0)
+        vec_quant(2, 0)
         h_quant(1, 1)
-        for cb in range(CB):
-            u_block(0, cb, bank_at(cb % 3))
-        turn_empty(2, 0)
-        turn_empty(3, 0)
-        e_scale_up(3, 1)
-        e_scale_up(0, 2)
+        u_block(0, 2)
+        u_block(0, 3)
+        turn_empty(0, 0, spare_bank())
+        turn_empty(0, 1, spare_bank())
+        e_scale_up(2, 1)
+        vec_quant(3, 0)
         u_quant(0)
+        e_scale_up(3, 1)
         for cb in range(CB):
-            u_block(1, cb, bank_at((cb + 1) % 3))
-        turn_empty(0, 0, 3)
-        turn_empty(0, 1, 4)
-        e_quant(1, 0)
-        e_quant(2, 0)
-        e_quant(3, 0)
-        e_scale_up(0, 3)
+            u_block(1, cb)
+        s_quant(0)
+        e_scale_up(0, 2)
         u_quant(1)
-        e_quant(0, 1)
-        turn_empty(1, 1, 5)
-        turn_empty(2, 1, 6)
-        turn_empty(3, 1, 7)
-        s_stage(0, 0, 3)
-        turn_empty(0, 2, 6)
-        turn_empty(0, 3, 4)
-        s_stage(0, 1, 7)
-        queue = [(m, rb + (4 if m == 0 else 2)) for rb in range(RB - 2) for m in range(M) if m > 0 or rb + 4 < RB]
+        e_scale_up(0, 3)
+        for m in VEC:
+            turn_empty(m, 1, spare_bank())
 
-        def next_scale_up():
+        queue = [(m, rb + (S_AHEAD if m == 0 else A_AHEAD)) for rb in range(RB - A_AHEAD) for m in range(M)
+                 if m > 0 or rb + S_AHEAD < RB]
+
+        def scale_next():
             if queue:
                 e_scale_up(*queue.pop(0))
 
-        for n in range(3):
-            next_scale_up()
-        s_product(0, 0)
-        if LH > 0:
-            s_affine(lin_b, "lin_b", 2, 3, 0, 0, on_vector=True)
-        next_scale_up()
-        e_quant(0, 3)
-        next_scale_up()
-        s_product(0, 1)
-        if LH > 1:
-            s_affine(lin_b, "lin_b", 2, 3, 0, 1, on_vector=True)
+        s_matmul(0, 0, S_BANK)
+        make_lin_s(0, 0)
+        make_lin_q(0, 0)
+        make_lin_t(0, 0)
+        e_turn(0, 2, bank_at(Q_THEN_UNIT))
+        e_turn(0, 3, bank_at(T_THEN_UNIT))
+        e_empty(0, 2)
+        e_empty(0, 3)
+        s_matmul(0, 1, UNIT_BANK)
+        make_lin_s(0, 1)
+        make_lin_q(0, 1)
+        make_lin_t(0, 1)
+        scale_next()
+        scale_next()
+        make_prod_s(0, 0)
+        scale_next()
+        s_quant(1)
+        scale_next()
+        make_prod_s(0, 1)
 
-        for rb in range(RB - 2):
+        for rb in range(RB - A_AHEAD):
             pair, half = rb // 2 + 1, rb % 2
-            has_unit = rb + 4 < RB
-            for m in range(1, M):
+            has_s_unit = rb + S_AHEAD < RB
+            ahead = rb + A_AHEAD
+            for m in VEC:
                 a_matmul(rb, m, m - 1)
                 square(rb, m)
-            s_matmul(pair, half, 3)
-            e_quant(1, rb + 1)
-            next_scale_up()
-            e_quant(2, rb + 1)
-            next_scale_up()
-            if has_unit:
-                turn_empty(0, rb + 4, 5)
-                s_linear(pair, half, (0,))
+            s_matmul(pair, half, S_BANK)
+            vec_quant(1, rb + 1)
+            scale_next()
+            vec_quant(2, rb + 1)
+            scale_next()
+            if rb == EXTRA_SCALE_AT:
+                scale_next()
+            if has_s_unit:
+                turn_empty(0, rb + S_AHEAD, bank_at(UNIT_THEN_B0))
+                make_lin_s(pair, half, (0,))
             else:
-                s_linear(pair, half)
-                s_affine(lin_q, "lin_q", 4, 5, pair, half, (0,))
-            t_turn(rb, 1, 4)
-            q_open(rb, 6)
-            t_turn(rb, 2)
-            t_turn(rb, 3)
-            b0_open(rb, 5)
-            e_turn(1, rb + 2, 7)
-            t_scale(rb)
-            t_product(rb)
-            if has_unit:
-                s_linear(pair, half, (1,))
+                make_lin_s(pair, half)
+                make_lin_q(pair, half, (0,))
+            t_turn(rb, 1, T_THEN_UNIT)
+            q_open(rb, Q_THEN_UNIT)
+            t_turn(rb, 2, T_THEN_UNIT)
+            t_turn(rb, 3, T_THEN_UNIT)
+            b0_open(rb, UNIT_THEN_B0, range(CB // 2), plain=True)
+            e_turn(1, ahead, bank_at(UNIT_BANK))
+            make_c6t(rb)
+            make_prod_t(rb)
+            if has_s_unit:
+                make_lin_s(pair, half, (1,))
             else:
-                s_affine(lin_q, "lin_q", 4, 5, pair, half, (1,))
-            s_product(pair, half)
-            moved = LB if LBF <= rb < RB - 3 else 0
-            s_affine(lin_b, "lin_b", 2, 3, pair, half, (0, 1)[:moved], on_vector=True)
-            e_empty(1, rb + 2)
-            e_quant(3, rb + 1)
+                make_lin_q(pair, half, (1,))
+            make_prod_s(pair, half)
+            e_empty(1, ahead)
+            vec_quant(3, rb + 1)
             q_close(rb)
+            b0_open(rb, UNIT_THEN_B0, range(CB // 2, CB), plain=True)
             q_empty(rb)
-            if rb + 3 < RB:
+            if ahead < RB - 1:
                 b0_close(rb)
-                if has_unit:
-                    s_affine(lin_q, "lin_q", 4, 5, pair, half)
-                s_affine(lin_b, "lin_b", 2, 3, pair, half, (0, 1)[moved:])
+                if has_s_unit:
+                    make_lin_q(pair, half)
+                make_lin_t(pair, half)
                 b0_store(rb)
-                for m in range(1, M):
+                for m in VEC:
                     b_store(rb, m)
-                turn_empty(2, rb + 2, 4)
-                turn_empty(3, rb + 2, 6)
-                if has_unit:
-                    e_quant(0, rb + 4)
-                next_scale_up()
+                turn_empty(2, ahead, bank_at(T_THEN_UNIT))
+                turn_empty(3, ahead, bank_at(Q_THEN_UNIT))
+                if has_s_unit and half == 1:
+                    s_quant(pair + 1)
+                scale_next()
             else:
-                turn_empty(2, rb + 2, 4)
-                turn_empty(3, rb + 2, 6)
+                turn_empty(2, ahead, bank_at(T_THEN_UNIT))
+                turn_empty(3, ahead, bank_at(Q_THEN_UNIT))
                 b0_close(rb)
-                e_quant(1, rb + 2)
                 b_store(rb, 1)
                 b_store(rb, 2)
-                e_quant(2, rb + 2)
+                vec_quant(1, ahead)
                 b_store(rb, 3)
-                e_quant(3, rb + 2)
+                vec_quant(2, ahead)
+                vec_quant(3, ahead)
                 b0_store(rb, nc.vector.tensor_copy)
-                s_affine(lin_b, "lin_b", 2, 3, pair, half, on_vector=True)
+                make_lin_t(pair, half, on_vector=True)
 
-        ra, rz = RB - 2, RB - 1
-        for m in range(1, M):
-            a_matmul(ra, m, m - 1)
-            square(ra, m)
-        a_matmul(rz, 1, 4)
-        for m in range(1, M):
-            t_turn(ra, m, 7)
-        a_matmul(rz, 2, 6)
-        a_matmul(rz, 3, 5)
-        for m in range(1, M):
-            square(rz, m)
-        t_scale(ra)
-        t_product(ra)
-        q_open(ra, 3)
-        q_close(ra)
-        q_empty(ra)
-        for m in range(1, M):
-            t_turn(rz, m, 7)
-        b_store(ra, 1)
-        b0_open(ra, 0)
-        b0_close(ra)
-        t_scale(rz)
-        q_open(rz, 3)
-        q_close(rz)
-        b_store(ra, 2)
-        b0_store(ra)
-        q_empty(rz)
-        t_product(rz)
-        b0_open(rz, 1)
-        b0_close(rz)
-        b_store(ra, 3)
-        b_store(rz, 1)
-        b0_store(rz)
-        b_store(rz, 2)
-        b_store(rz, 3)
+        rb_a, rb_b = RB - 2, RB - 1
+        for m in VEC:
+            a_matmul(rb_a, m, m - 1)
+            square(rb_a, m)
+        a_matmul(rb_b, 1, T_THEN_UNIT)
+        for m in VEC:
+            t_turn(rb_a, m, UNIT_BANK)
+        a_matmul(rb_b, 2, Q_THEN_UNIT)
+        a_matmul(rb_b, 3, UNIT_THEN_B0)
+        for m in VEC:
+            square(rb_b, m)
+        make_whole_q(rb_a)
+        make_prod_t(rb_a)
+        q_bank[rb_a] = bank_at(S_BANK)
+        q_close(rb_a, opens=True)
+        q_empty(rb_a)
+        for m in VEC:
+            t_turn(rb_b, m, UNIT_BANK)
+        b0_open(rb_a, S_BANK)
+        b0_close(rb_a)
+        make_c6t(rb_b)
+        b_store(rb_a, 1)
+        q_open(rb_b, 0)
+        q_close(rb_b)
+        b_store(rb_a, 2)
+        b0_store(rb_a)
+        make_prod_t(rb_b)
+        b_store(rb_a, 3)
+        q_empty(rb_b)
+        b0_open(rb_b, 1)
+        b0_close(rb_b)
+        b0_store(rb_b)
+        for m in VEC:
+            b_store(rb_b, m)

@@ -85,11 +85,11 @@ def tile_macedensitytricksymmetriccontraction_kernel(tc, h, w, e_bytes, e_scale,
 
         load_w(0)
         load_vec_bytes(0)
+        load_w(1)
         load_h(0, 0)
         load_h(0, 1)
-        load_w(1)
-        load_h(1, 0)
         load_s_bytes(0)
+        load_h(1, 0)
         load_h(1, 1)
         for rb in range(1, RB):
             load_vec_bytes(rb)
@@ -144,10 +144,10 @@ def tile_macedensitytricksymmetriccontraction_kernel(tc, h, w, e_bytes, e_scale,
 
         w_in, w_q, h_in, h_q, u_in, u_q = {}, {}, {}, {}, {}, {}
 
-        def w_interleave(g, copy):
+        def w_interleave(g):
             w_in[g] = keep.tile([P, PACK * C], BF16, name="w_in%d" % g, tag="wu_in%d" % g, align_bytes=64)
-            copy(out=w_in[g][:].rearrange("p (c i t) -> p c t i", i=4, t=PACK),
-                 in_=w_raw[g][:].rearrange("p t (c i) -> p c t i", i=4))
+            nc.scalar.copy(out=w_in[g][:].rearrange("p (c i t) -> p c t i", i=4, t=PACK),
+                           in_=w_raw[g][:].rearrange("p t (c i) -> p c t i", i=4))
 
         def w_quant(g):
             w_q[g] = quantize("w%d" % g, w_in[g][:])
@@ -318,18 +318,18 @@ def tile_macedensitytricksymmetriccontraction_kernel(tc, h, w, e_bytes, e_scale,
         nc.scalar.activation(out=coef_pad[0:J * CB, :], in_=coef_rows[:], func=ACT.Identity)
         spread_scale(0)
         spread_scale(1)
-        w_interleave(0, nc.scalar.copy)
+        w_interleave(0)
+        w_interleave(1)
         for m in VEC:
             e_scale_up(m, 0)
         w_quant(0)
-        turn_empty(1, 0, spare_bank())
         for t in range(PACK):
             h_slab(0, t)
-        h_quant(0, 0)
-        w_interleave(1, nc.vector.tensor_copy)
-        h_quant(0, 1)
         w_quant(1)
         e_scale_up(0, 0)
+        h_quant(0, 0)
+        h_quant(0, 1)
+        turn_empty(1, 0, spare_bank())
         turn_empty(2, 0, spare_bank())
         h_slab(1, 0)
         turn_coef()
@@ -471,7 +471,8 @@ def tile_macedensitytricksymmetriccontraction_kernel(tc, h, w, e_bytes, e_scale,
         q_empty(rb_a)
         for m in VEC:
             t_turn(rb_b, m, UNIT_BANK)
-        b0_open(rb_a, S_BANK)
+        b0_open(rb_a, S_BANK, range(CB // 2), plain=True)
+        b0_open(rb_a, S_BANK, range(CB // 2, CB))
         b0_close(rb_a)
         make_c6t(rb_b)
         b_store(rb_a, 1)

from contextlib import ExitStack

import concourse.mybir as mybir
from concourse.masks import make_identity

R, N, D, C, M, J = 1024, 1024, 1024, 512, 4, 7
FLOPS = 2 * N * D * C + 2 * M * R * N * C

F32 = mybir.dt.float32
BF16 = mybir.dt.bfloat16
U32 = mybir.dt.uint32
U8 = mybir.dt.uint8
FP8 = mybir.dt.float8_e4m3fn
FP8X4 = mybir.dt.float8_e4m3fn_x4
ALU = mybir.AluOpType
ACT = mybir.ActivationFunctionType

P = 128
PACK = 4
K_PASS = P * PACK
G = N // K_PASS
BANK = 512
CB = C // P
RB = R // P
VEC = range(1, M)

S_BANK = 3
T_THEN_UNIT = 4
UNIT_THEN_B0 = 5
Q_THEN_UNIT = 6
UNIT_BANK = 7
SPARE = (3, 4, 5, 6, 7)

A_AHEAD = 2
S_AHEAD = 4
SCALED_BUFS = 9
TURNED_BUFS = 6
CODE_BUFS = 9
EXTRA_SCALE_AT = 1


def tile_macedensitytricksymmetriccontraction_kernel(tc, h, w, e_bytes, e_scale, coef, out):
    nc = tc.nc
    with ExitStack() as ctx:
        keep = ctx.enter_context(tc.tile_pool(name="keep", bufs=1))
        work = ctx.enter_context(tc.tile_pool(name="work", bufs=2))
        psum = ctx.enter_context(tc.psum_pool(name="psum", bufs=1))
        ctx.enter_context(tc.manual_schedule())

        def cols(i, n):
            return slice(i * n, (i + 1) * n)

        def bank_at(i):
            return psum.tile([P, BANK], F32, name="bank%d" % i, tag="bank%d" % i)

        spare_taken = []

        def spare_bank():
            spare_taken.append(None)
            return bank_at(SPARE[len(spare_taken) % len(SPARE)])

        scale_col = keep.tile([P, G, PACK], F32, name="scale_col")
        nc.sync.dma_start(out=scale_col[:], in_=e_scale[0, 0, :].rearrange("(g p t) -> p g t", g=G, t=PACK))
        coef_rows = keep.tile([J * CB, P], BF16, name="coef_rows")
        nc.sync.dma_start(out=coef_rows[:], in_=coef.rearrange("j (b p) -> (j b) p", p=P))

        w_raw, h_raw, vec_bytes, s_bytes = {}, {}, {}, {}

        def load_w(g):
            w_raw[g] = keep.tile([P, PACK, C], BF16, name="w_raw%d" % g)
            nc.sync.dma_start(out=w_raw[g][:], in_=w[cols(g, K_PASS), :].rearrange("(p t) c -> p t c", t=PACK))

        def load_h(g, half):
            h_raw[g, half] = keep.tile([P, 2 * D], BF16, name="h_raw%d_%d" % (g, half))
            rows = h[cols(g, K_PASS), :].rearrange("(p s t) d -> p s (t d)", s=2, t=2)
            nc.sync.dma_start(out=h_raw[g, half][:], in_=rows[:, half, :])

        def load_vec_bytes(rb):
            vec_bytes[rb] = keep.tile([P, M - 1, N], U8, name="vec_bytes%d" % rb)
            nc.sync.dma_start(out=vec_bytes[rb][:], in_=e_bytes[1:M, cols(rb, P), :].rearrange("m r k -> r m k"))

        def load_s_bytes(pair):
            s_bytes[pair] = keep.tile([P, 2, N], U8, name="s_bytes%d" % pair)
            nc.sync.dma_start(out=s_bytes[pair][:], in_=e_bytes[0, cols(pair, 2 * P), :].rearrange("(b r) k -> r b k", b=2))

        load_w(0)
        load_vec_bytes(0)
        load_w(1)
        load_h(0, 0)
        load_h(0, 1)
        load_s_bytes(0)
        load_h(1, 0)
        load_h(1, 1)
        for rb in range(1, RB):
            load_vec_bytes(rb)
            if rb < RB // 2:
                load_s_bytes(rb)

        ident = keep.tile([P, P], F32, name="ident")
        make_identity(nc, ident[:])
        coef_pad = keep.tile([P, P], F32, name="coef_pad")
        scale_row = keep.tile([P, N], F32, name="scale_row")
        coef_col = keep.tile([P, J * CB], F32, name="coef_col")

        def spread_scale(g):
            bank = spare_bank()
            for t in range(PACK):
                nc.tensor.transpose(bank[:, cols(t, P)], scale_col[:, g, t:t + 1].to_broadcast([P, P]), ident[:])
            nc.vector.tensor_copy(out=scale_row[:, cols(g, K_PASS)].rearrange("q (p t) -> q p t", t=PACK),
                                  in_=bank[:].rearrange("q (t p) -> q p t", t=PACK))

        def turn_coef():
            bank = spare_bank()
            nc.tensor.matmul(bank[:, 0:P], coef_pad[:], ident[:], start=True, stop=True, is_transpose=False)
            nc.vector.tensor_copy(out=coef_col[:], in_=bank[:, 0:J * CB])

        def cf(j, cb):
            return coef_col[:, j * CB + cb:j * CB + cb + 1]

        def quantize(name, src, bufs=1):
            width = src.shape[1] // PACK
            codes = keep.tile([P, width], U32, name=name + "_codes", tag=name + "_codes", bufs=bufs, align_bytes=64)
            scales = keep.tile([P, width], U8, name=name + "_scales", tag=name + "_scales", bufs=bufs, align_bytes=64)
            nc.vector.quantize_mx(out=codes[:].bitcast(FP8X4), scales=scales[:], in_=src)
            return codes, scales

        def mx(dst, lhs, lcols, rhs, rcols, g):
            nc.tensor.matmul_mx(out=dst, lhsT=lhs[0][:, lcols].bitcast(FP8X4), lhsT_scale=lhs[1][:, lcols],
                                rhs=rhs[0][:, rcols].bitcast(FP8X4), rhs_scale=rhs[1][:, rcols],
                                start=(g == 0), stop=(g == G - 1))

        def turn_rows(rows, bank):
            words = rows.bitcast(F32)
            for g in range(G):
                for u in range(2):
                    nc.tensor.transpose(bank[:, cols(2 * g + u, P)], words[:, 2 * P * g + u:2 * P * (g + 1):2], ident[:])
            return bank

        def as_words(tile):
            return tile.bitcast(F32).rearrange("p (g r u) -> p g r u", g=G, u=2)

        def empty_turned(bank, dst_words):
            nc.scalar.copy(out=dst_words, in_=bank[:].rearrange("p (g u r) -> p g r u", g=G, u=2))

        w_in, w_q, h_in, h_q, u_in, u_q = {}, {}, {}, {}, {}, {}

        def w_interleave(g):
            w_in[g] = keep.tile([P, PACK * C], BF16, name="w_in%d" % g, tag="wu_in%d" % g, align_bytes=64)
            nc.scalar.copy(out=w_in[g][:].rearrange("p (c i t) -> p c t i", i=4, t=PACK),
                           in_=w_raw[g][:].rearrange("p t (c i) -> p c t i", i=4))

        def w_quant(g):
            w_q[g] = quantize("w%d" % g, w_in[g][:])

        def h_slab(g, t):
            if t % 2 == 0:
                h_in[g, t // 2] = keep.tile([P, 2 * D], BF16, name="h_in%d_%d" % (g, t // 2), align_bytes=64)
            bank = turn_rows(h_raw[g, t // 2][:, cols(t % 2, D)], spare_bank())
            empty_turned(bank, as_words(h_in[g, t // 2][:, cols(t % 2, D)]))

        def h_quant(g, half):
            h_q[g, half] = quantize("h%d_%d" % (g, half), h_in[g, half][:])

        def u_block(g, cb):
            bank = bank_at((g * CB + cb) % 3)
            if cb == 0:
                u_in[g] = keep.tile([P, PACK * C], BF16, name="u_in%d" % g, tag="wu_in%d" % g, align_bytes=64)
            for t in range(PACK):
                for dg in range(G):
                    mx(bank[:, cols(t, P)], h_q[g, t // 2], cols((t % 2) * G + dg, P), w_q[dg], cols(cb, P), dg)
            nc.scalar.copy(out=u_in[g][:, cols(cb, PACK * P)].rearrange("p (c t) -> p c t", t=PACK),
                           in_=bank[:].rearrange("p (t c) -> p c t", t=PACK))

        def u_quant(g):
            u_q[g] = quantize("u%d" % g, u_in[g][:])

        e_val, e_bank, e_in, vec_q, s_q = {}, {}, {}, {}, {}

        def e_scale_up(m, rb):
            src = s_bytes[rb // 2][:, rb % 2, :] if m == 0 else vec_bytes[rb][:, m - 1, :]
            e_val[m, rb] = work.tile([P, N], BF16, name="e_val", tag="e_val", bufs=SCALED_BUFS)
            nc.vector.tensor_tensor(out=e_val[m, rb][:], in0=src.bitcast(FP8), in1=scale_row[:], op=ALU.mult)

        def e_turn(m, rb, bank):
            e_bank[m, rb] = turn_rows(e_val[m, rb][:], bank)

        def e_empty(m, rb):
            if m == 0:
                if rb % 2 == 0:
                    e_in[0, rb // 2] = work.tile([P, 2 * N], BF16, name="s_in", tag="s_in", align_bytes=64)
                dst = as_words(e_in[0, rb // 2][:])[:, :, cols(rb % 2, P), :]
            else:
                e_in[m, rb] = work.tile([P, N], BF16, name="vec_in", tag="vec_in", bufs=TURNED_BUFS, align_bytes=64)
                dst = as_words(e_in[m, rb][:])
            empty_turned(e_bank[m, rb], dst)

        def turn_empty(m, rb, bank):
            e_turn(m, rb, bank)
            e_empty(m, rb)

        def vec_quant(m, rb):
            vec_q[m, rb] = quantize("vec", e_in[m, rb][:], CODE_BUFS)

        def s_quant(pair):
            s_q[pair] = quantize("s", e_in[0, pair][:], 2)

        s_bank, lin_s, lin_t, lin_q, prod_s = {}, {}, {}, {}, {}

        def s_matmul(pair, half, at):
            s_bank[pair, half] = bank_at(at)
            for b in range(2):
                for g in range(G):
                    mx(s_bank[pair, half][:, cols(b, 2 * P)], u_q[g], cols(2 * half + b, P), s_q[pair], cols(g, 2 * P), g)

        def affine(dst, j, pair, half, b, on_vector):
            src, cb = s_bank[pair, half][:, cols(b, 2 * P)], 2 * half + b
            if on_vector:
                nc.vector.tensor_scalar(out=dst, in0=src, scalar1=cf(j + 1, cb), scalar2=cf(j, cb), op0=ALU.mult, op1=ALU.add)
            else:
                nc.scalar.activation(out=dst, in_=src, func=ACT.Identity, scale=cf(j + 1, cb), bias=cf(j, cb))

        def pair_block(store, name, pair, cb):
            if cb == 0:
                store[pair] = work.tile([P, CB, 2 * P], F32, name=name, tag=name)
            return store[pair][:, cb, :]

        def make_lin_s(pair, half, blocks=(0, 1)):
            for b in blocks:
                if b == 0:
                    lin_s[pair, half] = work.tile([P, BANK], F32, name="lin_s", tag="lin_s")
                affine(lin_s[pair, half][:, cols(b, 2 * P)], 0, pair, half, b, False)

        def make_lin_t(pair, half, on_vector=False):
            for b in range(2):
                affine(pair_block(lin_t, "lin_t", pair, 2 * half + b), 2, pair, half, b, on_vector)

        def make_lin_q(pair, half, blocks=(0, 1)):
            for b in blocks:
                affine(pair_block(lin_q, "lin_q", pair, 2 * half + b), 4, pair, half, b, False)

        def make_prod_s(pair, half):
            if half == 0:
                prod_s[pair] = work.tile([P, CB, 2 * P], F32, name="prod_s", tag="prod_s")
            dst = prod_s[pair][:, cols(half, 2), :].rearrange("p b r -> p (b r)")
            nc.vector.tensor_tensor(out=dst, in0=s_bank[pair, half][:], in1=lin_s[pair, half][:], op=ALU.mult)

        def piece(store, rb, cb):
            return store[rb // 2][:, cb, cols(rb % 2, P)]

        am, sq, t_bank, q_term, prod_t, q_bank, b0_bank, q_row = {}, {}, {}, {}, {}, {}, {}, {}

        def a_matmul(rb, m, at):
            am[rb, m] = bank_at(at)
            for g in range(G):
                mx(am[rb, m][:], vec_q[m, rb], cols(g, P), u_q[g], cols(0, C), g)

        def square(rb, m):
            sq[rb, m] = work.tile([P, C], F32, name="sq%d" % m, tag="sq%d" % m)
            nc.scalar.activation(out=sq[rb, m][:], in_=am[rb, m][:], func=ACT.Square, scale=3.0 ** -0.5)

        def turn_add(bank, part, first, last, blocks=range(CB), plain=False):
            for cb in blocks:
                nc.tensor.matmul(bank[:, cols(cb, P)], part(cb), ident[:], start=(first and cb == 0),
                                 stop=(last and cb == CB - 1), is_transpose=(not plain))

        def t_turn(rb, m, at):
            if m == 1:
                t_bank[rb] = bank_at(at)
            turn_add(t_bank[rb], lambda cb: sq[rb, m][:, cols(cb, P)], m == 1, m == M - 1)

        def make_c6t(rb):
            q_term[rb] = work.tile([P, C], F32, name="q_term", tag="q_term")
            for cb in range(CB):
                nc.scalar.activation(out=q_term[rb][:, cols(cb, P)], in_=t_bank[rb][:, cols(cb, P)], func=ACT.Copy, scale=cf(6, cb))

        def make_whole_q(rb):
            q_term[rb] = work.tile([P, C], F32, name="q_term", tag="q_term")
            for cb in range(CB):
                nc.vector.scalar_tensor_tensor(out=q_term[rb][:, cols(cb, P)], in0=t_bank[rb][:, cols(cb, P)], scalar=cf(6, cb),
                                               in1=piece(lin_q, rb, cb), op0=ALU.mult, op1=ALU.add)

        def make_prod_t(rb):
            prod_t[rb] = work.tile([P, C], F32, name="prod_t", tag="prod_t")
            nc.vector.tensor_tensor(out=prod_t[rb][:].rearrange("p (b r) -> p b r", b=CB),
                                    in0=t_bank[rb][:].rearrange("p (b r) -> p b r", b=CB),
                                    in1=lin_t[rb // 2][:, :, cols(rb % 2, P)], op=ALU.mult)

        def q_open(rb, at):
            q_bank[rb] = bank_at(at)
            turn_add(q_bank[rb], lambda cb: piece(lin_q, rb, cb), True, False)

        def q_close(rb, opens=False):
            turn_add(q_bank[rb], lambda cb: q_term[rb][:, cols(cb, P)], opens, True)

        def b0_open(rb, at, blocks=range(CB), plain=False):
            if 0 in blocks:
                b0_bank[rb] = bank_at(at)
            turn_add(b0_bank[rb], lambda cb: piece(prod_s, rb, cb), True, False, blocks, plain)

        def b0_close(rb):
            turn_add(b0_bank[rb], lambda cb: prod_t[rb][:, cols(cb, P)], False, True)

        def q_empty(rb):
            q_row[rb] = work.tile([P, C], F32, name="q_row", tag="q_row")
            nc.scalar.copy(out=q_row[rb][:], in_=q_bank[rb][:])

        def b0_store(rb, copy=nc.scalar.copy):
            res = work.tile([P, C], F32, name="res0", tag="res0")
            copy(out=res[:], in_=b0_bank[rb][:])
            nc.sync.dma_start(out=out[0, cols(rb, P), :], in_=res[:])

        def b_store(rb, m):
            res = work.tile([P, C], F32, name="res%d" % m, tag="res%d" % m)
            nc.vector.tensor_tensor(out=res[:], in0=am[rb, m][:], in1=q_row[rb][:], op=ALU.mult)
            nc.sync.dma_start(out=out[m, cols(rb, P), :], in_=res[:])

        nc.vector.memset(coef_pad[:], 0.0)
        nc.scalar.activation(out=coef_pad[0:J * CB, :], in_=coef_rows[:], func=ACT.Identity)
        spread_scale(0)
        spread_scale(1)
        w_interleave(0)
        w_interleave(1)
        for m in VEC:
            e_scale_up(m, 0)
        w_quant(0)
        for t in range(PACK):
            h_slab(0, t)
        w_quant(1)
        e_scale_up(0, 0)
        h_quant(0, 0)
        h_quant(0, 1)
        turn_empty(1, 0, spare_bank())
        turn_empty(2, 0, spare_bank())
        h_slab(1, 0)
        turn_coef()
        h_slab(1, 1)
        turn_empty(3, 0, spare_bank())
        e_scale_up(0, 1)
        h_quant(1, 0)
        u_block(0, 0)
        u_block(0, 1)
        h_slab(1, 2)
        h_slab(1, 3)
        e_scale_up(1, 1)
        vec_quant(1, 0)
        vec_quant(2, 0)
        h_quant(1, 1)
        u_block(0, 2)
        u_block(0, 3)
        turn_empty(0, 0, spare_bank())
        turn_empty(0, 1, spare_bank())
        e_scale_up(2, 1)
        vec_quant(3, 0)
        u_quant(0)
        e_scale_up(3, 1)
        for cb in range(CB):
            u_block(1, cb)
        s_quant(0)
        e_scale_up(0, 2)
        u_quant(1)
        e_scale_up(0, 3)
        for m in VEC:
            turn_empty(m, 1, spare_bank())

        queue = [(m, rb + (S_AHEAD if m == 0 else A_AHEAD)) for rb in range(RB - A_AHEAD) for m in range(M)
                 if m > 0 or rb + S_AHEAD < RB]

        def scale_next():
            if queue:
                e_scale_up(*queue.pop(0))

        s_matmul(0, 0, S_BANK)
        make_lin_s(0, 0)
        make_lin_q(0, 0)
        make_lin_t(0, 0)
        e_turn(0, 2, bank_at(Q_THEN_UNIT))
        e_turn(0, 3, bank_at(T_THEN_UNIT))
        e_empty(0, 2)
        e_empty(0, 3)
        s_matmul(0, 1, UNIT_BANK)
        make_lin_s(0, 1)
        make_lin_q(0, 1)
        make_lin_t(0, 1)
        scale_next()
        scale_next()
        make_prod_s(0, 0)
        scale_next()
        s_quant(1)
        scale_next()
        make_prod_s(0, 1)

        for rb in range(RB - A_AHEAD):
            pair, half = rb // 2 + 1, rb % 2
            has_s_unit = rb + S_AHEAD < RB
            ahead = rb + A_AHEAD
            for m in VEC:
                a_matmul(rb, m, m - 1)
                square(rb, m)
            s_matmul(pair, half, S_BANK)
            vec_quant(1, rb + 1)
            scale_next()
            vec_quant(2, rb + 1)
            scale_next()
            if rb == EXTRA_SCALE_AT:
                scale_next()
            if has_s_unit:
                turn_empty(0, rb + S_AHEAD, bank_at(UNIT_THEN_B0))
                make_lin_s(pair, half, (0,))
            else:
                make_lin_s(pair, half)
                make_lin_q(pair, half, (0,))
            t_turn(rb, 1, T_THEN_UNIT)
            q_open(rb, Q_THEN_UNIT)
            t_turn(rb, 2, T_THEN_UNIT)
            t_turn(rb, 3, T_THEN_UNIT)
            b0_open(rb, UNIT_THEN_B0, range(CB // 2), plain=True)
            e_turn(1, ahead, bank_at(UNIT_BANK))
            make_c6t(rb)
            make_prod_t(rb)
            if has_s_unit:
                make_lin_s(pair, half, (1,))
            else:
                make_lin_q(pair, half, (1,))
            make_prod_s(pair, half)
            e_empty(1, ahead)
            vec_quant(3, rb + 1)
            q_close(rb)
            b0_open(rb, UNIT_THEN_B0, range(CB // 2, CB), plain=True)
            q_empty(rb)
            if ahead < RB - 1:
                b0_close(rb)
                if has_s_unit:
                    make_lin_q(pair, half)
                make_lin_t(pair, half)
                b0_store(rb)
                for m in VEC:
                    b_store(rb, m)
                turn_empty(2, ahead, bank_at(T_THEN_UNIT))
                turn_empty(3, ahead, bank_at(Q_THEN_UNIT))
                if has_s_unit and half == 1:
                    s_quant(pair + 1)
                scale_next()
            else:
                turn_empty(2, ahead, bank_at(T_THEN_UNIT))
                turn_empty(3, ahead, bank_at(Q_THEN_UNIT))
                b0_close(rb)
                b_store(rb, 1)
                b_store(rb, 2)
                vec_quant(1, ahead)
                b_store(rb, 3)
                vec_quant(2, ahead)
                vec_quant(3, ahead)
                b0_store(rb, nc.vector.tensor_copy)
                make_lin_t(pair, half, on_vector=True)

        rb_a, rb_b = RB - 2, RB - 1
        for m in VEC:
            a_matmul(rb_a, m, m - 1)
            square(rb_a, m)
        a_matmul(rb_b, 1, T_THEN_UNIT)
        for m in VEC:
            t_turn(rb_a, m, UNIT_BANK)
        a_matmul(rb_b, 2, Q_THEN_UNIT)
        a_matmul(rb_b, 3, UNIT_THEN_B0)
        for m in VEC:
            square(rb_b, m)
        make_whole_q(rb_a)
        make_prod_t(rb_a)
        q_bank[rb_a] = bank_at(S_BANK)
        q_close(rb_a, opens=True)
        q_empty(rb_a)
        for m in VEC:
            t_turn(rb_b, m, UNIT_BANK)
        b0_open(rb_a, S_BANK, range(CB // 2), plain=True)
        b0_open(rb_a, S_BANK, range(CB // 2, CB))
        b0_close(rb_a)
        make_c6t(rb_b)
        b_store(rb_a, 1)
        q_open(rb_b, 0)
        q_close(rb_b)
        b_store(rb_a, 2)
        b0_store(rb_a)
        make_prod_t(rb_b)
        b_store(rb_a, 3)
        q_empty(rb_b)
        b0_open(rb_b, 1)
        b0_close(rb_b)
        b0_store(rb_b)
        for m in VEC:
            b_store(rb_b, m)
